import numpy as np, ml_dtypes
CORES = [3,11,19,27,35,43,51,59]
N = 8
BF = ml_dtypes.bfloat16
S, R, NF, PH, LB, RO = 1024, 8192, 512, 1024, 10, 3
def place(s, p):
    return ((s * p >> 4) + s + 37 * p) & (R - 1)
def records(rng):
    st = ((np.arange(8)[None, :] + rng.integers(0, 3, (N, 1))) % 3)[:, :, None, None]
    lo = np.where(st == 0, 0, np.where(st == 1, 64 * rng.integers(0, 4, (N, 8, 1, R)), 200 * (rng.random((N, 8, 1, R)) < 0.35))).astype(np.int32)
    span = np.where(st == 0, 256, np.where(st == 1, 64, 56)).astype(np.float32)
    x = np.minimum(lo + (rng.random((N, 8, 16, R), dtype=np.float32) * span).astype(np.int32), 255)
    u = rng.random((N, 8, 16, 1))
    th = np.where(st == 0, 1000 + 700 * u, np.where(st == 1, 256 + 2000 * u, 450 + 1150 * u)).astype(np.int64)
    return x, th
def parts(rng):
    var = rng.choice(np.array([0.2, 0.35, 0.5]), (N, 8, 1, 1)); emp = rng.choice(np.array([0.2, 0.45, 0.7]), (N, 8, 1, 1))
    tk = rng.integers(0, S, (N, 8, 16, S)) + S * (rng.random((N, 8, 16, S)) < var)
    fr = np.where(rng.random((N, 8, 16, NF)) < emp, -1, rng.integers(0, S * PH, (N, 8, 16, NF)))
    return tk, fr, rng.integers(0, S, (N, 8, NF)), rng.integers(0, NF, (N, 8, NF)), rng.integers(0, S, (N, 8, NF))
def pack(x, tk, fr, th, s, f, c):
    return {"x": np.ascontiguousarray(x.reshape(N, 128, R)).astype(np.float32).astype(BF), "sk": np.ascontiguousarray(tk.reshape(N, 128, S)).astype(np.int32),
            "fr": np.ascontiguousarray(fr.reshape(N, 128, NF)).astype(np.int32), "th": np.ascontiguousarray(th.reshape(N, 128, 1)).astype(np.int32),
            "gs": s.astype(np.int32), "gf": f.astype(np.int32), "gcl": c.astype(np.int32)}
def setup_inputs(rng):
    x, th = records(rng); tk, fr, s, f, c = parts(rng)
    return pack(x, tk, fr, th, s, f, c)
def setup_inputs_spread(rng):
    amp = np.exp2(8 * rng.random((N, 8, 1, R))).astype(np.float32)
    x = np.minimum((rng.random((N, 8, 16, R), dtype=np.float32) * amp).astype(np.int32), 255)
    x = np.where(rng.random((N, 8, 1, R)) < 0.0625, 255 - x, x)
    th = np.minimum(np.exp2(12 * rng.random((N, 8, 16, 1))).astype(np.int64), 4080)
    u = rng.random((N, 8, 16, S)); tk = np.minimum((2 * S * u * np.sqrt(u)).astype(np.int64), 2 * S - 1)
    v = rng.random((N, 8, 16, NF)); fr = np.where(rng.random(v.shape) < 0.3 * rng.random((N, 8, 1, 1)) + 0.1, -1, np.minimum((S * PH * v * v).astype(np.int64), S * PH - 1))
    w = rng.random((3, N, 8, NF)); w = w * w
    return pack(x, tk, fr, th, np.minimum((S * w[0]).astype(np.int64), S - 1), np.minimum((NF * w[1]).astype(np.int64), NF - 1), np.minimum((S * w[2]).astype(np.int64), S - 1))
def setup_inputs_ends(rng):
    one = rng.random((N, 8, 1, R)) < 0.5; each = rng.random((N, 8, 16, R)) < 0.5
    x = 255 * np.where(rng.random((N, 8, 1, R)) < 0.25, each, one).astype(np.int64)
    tk = (2 * S - 1) * rng.integers(0, 2, (N, 8, 16, S)); fr = np.where(rng.integers(0, 2, (N, 8, 16, NF)) == 1, S * PH - 1, -1)
    s = (S - 1) * rng.integers(0, 2, (N, 8, NF)); f = (NF - 1) * rng.integers(0, 2, (N, 8, NF)); c = (S - 1) * rng.integers(0, 2, (N, 8, NF))
    th = np.full((N, 8, 16, 1), 4080, np.int64)
    for a in range(N):
        for g in range(8):
            if g == 7: z = rng.permutation(15)[:9 if a % 2 == 0 else 7]
            else: z = rng.permutation(16)[:16 if g == 6 else 8]
            th[a, g, z, 0] = 0
    s[:, :, NF - 1] = S - 1; f[:, :, NF - 1] = NF - 1; c[:, :, NF - 1] = 0
    tk[::2, :, :, S - 1] = 2 * S - 1; tk[::2, :, :, 0] = 0; tk[:, 7, :, S - 1] = 2 * S - 1; tk[:, 7, :, 0] = 0
    x[..., place(S - 1, PH - 1)] = 255; x[..., place(S - 1, NF - 1)] = 255; x[..., place(0, NF - 1)] = 0
    return pack(x, tk, fr, th, s, f, c)
def setup_inputs_corners(rng):
    x, th = records(rng); tk, fr, s, f, c = parts(rng); i = np.arange(NF); even = i % 2 == 0
    near = np.array([[3, 21], [21, 3], [5, 19], [19, 5], [7, 9], [9, 7]])
    for a in range(N):
        o = rng.permutation(8)
        tk[a, o[0]] = tk[a, o[0]] & (S - 1); fr[a, o[0]] = -1
        tk[a, o[1]] = (tk[a, o[1]] & (S - 1)) + S; fr[a, o[1]] = -1
        tk[a, o[2]] = (tk[a, o[2]] & (S - 1)) + S
        fr[a, o[2]] = PH * rng.integers(0, S, (16, NF)) + np.where(rng.random((16, NF)) < 0.5, i, NF + i)
        f[a, o[3]] = i; fr[a, o[3]] = np.where(i % 2 == 0, -1, rng.integers(0, S * PH, (16, NF)))
        f[a, o[4]] = rng.choice(np.array([0, NF - 1]), NF); s[a, o[4]] = rng.choice(np.array([0, S - 1]), NF); c[a, o[4]] = np.where(rng.random(NF) < 0.5, s[a, o[4]], S - 1 - s[a, o[4]])
        fr[a, o[4]] = np.where(rng.random((16, NF)) < 0.4, -1, PH * rng.choice(np.array([0, S - 1]), (16, NF)) + rng.choice(np.array([0, NF - 1, NF, PH - 1]), (16, NF)))
        th[a, o[5]] = 4080; th[a, o[6]] = 0; th[a, o[7]] = 4080; th[a, o[7], rng.permutation(16)[:8]] = 0
        f[a, o[5]] = np.where(even, i, f[a, o[5]]); c[a, o[5]] = np.where(even, s[a, o[5]], c[a, o[5]]); fr[a, o[5]] = np.where(even, -1, fr[a, o[5]])
        pq = near[rng.integers(0, 6, NF)]
        s[a, o[6]] = np.where(even, S - pq[:, 0], s[a, o[6]]); c[a, o[6]] = np.where(even, S - pq[:, 1], c[a, o[6]])
    return pack(x, tk, fr, th, s, f, c)
def setup_inputs_ties(rng):
    v, th = records(rng); tk, fr, s, f, c = parts(rng)
    x = np.broadcast_to(60 * rng.integers(0, 5, (N, 8, 1, R)), (N, 8, 16, R)).copy()
    th = rng.choice(np.array([959, 960, 961, 1919, 1920, 1921]), (N, 8, 16, 1))
    off = rng.integers(0, 4, (N, 2, 16, R)) * (rng.random((N, 2, 1, R)) < 0.5)
    x[:, 1::4] = np.abs(255 * rng.integers(0, 2, (N, 2, 1, R)) - off)
    lev = np.array([0, 0, 0, 24, 24, 24, 4048, 4056, 4060, 4064, 4078, 4079, 4079, 4079, 4080, 4080])
    th[:, 1::4] = lev[np.argsort(rng.random((N, 2, 16, 1)), axis=2)]
    few = rng.integers(0, S, (N, 4, 3)); which = rng.integers(0, 3, (2, N, 4, NF))
    s[:, ::2] = np.take_along_axis(few, which[0], 2); c[:, ::2] = np.take_along_axis(few, which[1], 2); f[:, ::2] = rng.integers(0, 4, (N, 4, NF))
    return pack(x, tk, fr, th, s, f, c)
def check_inputs(d):
    bad = []
    for k, lo, hi in (("x", 0, 255), ("sk", 0, 2 * S - 1), ("fr", -1, S * PH - 1), ("th", 0, 4080), ("gs", 0, S - 1), ("gf", 0, NF - 1), ("gcl", 0, S - 1)):
        if k not in d: bad.append("no " + k); continue
        v = np.asarray(d[k]).astype(np.float64)
        if not (np.min(v) >= lo and np.max(v) <= hi): bad.append("range of " + k)
        elif np.any(v != np.floor(v)): bad.append("whole numbers in " + k)
    return bad
def reference(x, sk, fr, th, gs, gf, gcl):
    X = x.astype(np.float32).astype(np.int32).reshape(N, 8, 16, R); T = sk.astype(np.int64).reshape(N, 8, 16, S); lim = th.astype(np.int64).reshape(N, 8, 16, 1)
    own = fr.astype(np.int64).reshape(N, 8, 16, NF); F = np.concatenate([own, own], axis=3)
    i = np.arange(NF); mark = np.zeros((N, 8, 16, NF), bool); A = np.zeros((N, NF), np.int64)
    s = gs.astype(np.int64); f = gf.astype(np.int64); c = gcl.astype(np.int64); h = np.zeros_like(s) + i
    s0 = s; f0 = f; c0 = c
    def molecules(a, b):
        v = np.take_along_axis(T, a[:, :, None, :], 3); w = np.take_along_axis(F, b[:, :, None, :], 3)
        return np.where((v >= S) & (w >= 0), w, (v & (S - 1)) * PH + b[:, :, None, :]), (v >= S) & (w < 0)
    def pick(m):
        return np.take_along_axis(X, place(m >> LB, m & (PH - 1)).reshape(N, 8, 1, 16 * NF), 3)
    for rnd in range(RO):
        goal, _ = molecules(s, f); clause, hole = molecules(c, h)
        free = hole & (h == i)[:, :, None, :]; clause = np.where(free, goal, clause)
        D = np.add.reduce(np.abs(pick(goal) - pick(clause)), axis=2).astype(np.int64).reshape(N, 8, 16, NF)
        over = D > lim; clash = np.add.reduce(over.astype(np.int64), axis=2) >= 8 + (A & 1)[:, None, :]
        m = np.argmax(np.where(over, -1, D), axis=2)[:, :, None, :]
        gm = np.take_along_axis(goal, m, 2)[:, :, 0]; cm = np.take_along_axis(clause, m, 2)[:, :, 0]
        dm = np.take_along_axis(D, m, 2)[:, :, 0]; tm = np.take_along_axis(np.broadcast_to(lim, D.shape), m, 2)[:, :, 0]
        save = ~clash & (2 * dm < tm)
        bind = free & ~clash[:, :, None, :]
        own = np.where(mark & clash[:, :, None, :], -1, np.where(bind, goal, own))
        mark = (mark | bind) & ~(clash | save)[:, :, None, :]
        nxt = ((c0 * s0 >> 5) + c0 + 1) & (S - 1)
        s = np.where(clash, s0, gm >> LB); f = np.where(clash, f0, gm & (PH - 1))
        c = np.where(clash, nxt, cm >> LB); h = np.where(clash, i, cm & (PH - 1))
        s0 = np.where(save, s, s0); f0 = np.where(save, f, f0); c0 = np.where(clash, nxt, np.where(save, c, c0))
        A = np.add.reduce(clash.astype(np.int64), axis=1)
        F = np.concatenate([own, F[..., NF:]], axis=3)
        if rnd < RO - 1:
            d = 1 + rnd % (N - 1); col = np.take_along_axis(F, f[:, :, None, :], 3)
            F = np.concatenate([own, np.roll(col, d, axis=0)], axis=3); s = np.roll(s, d, axis=0); f = np.zeros_like(s) + NF + i
    return {"yf": np.where(own < 0, -1, 2 * own + mark).reshape(N, 128, NF).astype(np.float32), "yg": (PH * s + f).astype(np.float32), "yc": (PH * c + h).astype(np.float32),
            "ysg": (PH * s0 + f0).astype(np.float32), "yk": c0.astype(np.float32)}

@@ -1,0 +1,526 @@
+from concourse.mybir import AluOpType, ActivationFunctionType
+A = AluOpType
+F = ActivationFunctionType
+C0 = 592 * 2048 + 16
+CH = ((0, 256), (256, 384), (384, 512))
+MV = ((0, 256), (256, 512))
+def _sb(names, shape, d):
+    return {n: ("sbuf", shape, d) for n in names.split()}
+SCRATCH = {"xr": ("sbuf", [128, 8192], "bfloat16"), "T1": ("sbuf", [128, 1024], "float32"), "FB": ("sbuf", [128, 2560], "float32"),
+           "PR": ("sbuf", [128, 1024], "int32"), "OI": ("sbuf", [128, 1024], "int32"), "Z": ("sbuf", [128, 2048], "float16"),
+           "Ib": ("sbuf", [128, 1280], "bfloat16"), "BO": ("sbuf", [128, 384], "bfloat16"), "BY": ("sbuf", [128, 2048], "bfloat16"),
+           "row": ("sbuf", [128, 1664], "bfloat16"), "it": ("sbuf", [128, 640], "int32"), "il": ("sbuf", [128, 128], "int32"),
+           "If": ("sbuf", [128, 128], "float32"), "E8": ("sbuf", [128, 128], "bfloat16"), "seg": ("sbuf", [128, 256], "float32"),
+           "thi": ("sbuf", [128, 1], "int32"), "th2": ("sbuf", [128, 8], "float32"), "M16": ("sbuf", [128, 16], "float32"),
+           "Ex": ("sbuf", [128, 16], "uint16"), "lst": ("sbuf", [128, 1536], "int32"), "lsh": ("sbuf", [128, 1536], "float16"),
+           "skb": ("sbuf", [128, 1024], "int32"), "skh": ("sbuf", [128, 1024], "float16"), "skv": ("sbuf", [128, 1024], "bfloat16"),
+           "OUT": ("sbuf", [128, 2048], "float32"), "fo": ("sbuf", [128, 128], "float16"), "fi": ("sbuf", [128, 128], "float16"),
+           "Vm": ("sbuf", [128, 144], "bfloat16"), "V8": ("sbuf", [128, 144], "bfloat16")}
+SCRATCH.update(_sb("U Df", [128, 8192], "bfloat16"))
+SCRATCH.update(_sb("AG AC bR cand keep Dc Mx kS col CI CB yv mf", [128, 512], "float32"))
+SCRATCH.update(_sb("XG XC EG PG QG PC QC frb ai oi lo", [128, 512], "int32"))
+SCRATCH.update(_sb("OG OC", [128, 512], "uint16"))
+SCRATCH.update(_sb("nfr mu sgn sg2 sc a2 oh zb", [128, 512], "bfloat16"))
+SCRATCH.update(_sb("SF0 NXH cl2 dd SF cz CM CHd zz tq nx", [128, 64], "float32"))
+SCRATCH.update(_sb("IL CP0 m1", [128, 32], "float32"))
+SCRATCH.update(_sb("nxi fxi", [128, 32], "int32"))
+SCRATCH.update(_sb("eqb", [128, 32], "bfloat16"))
+SCRATCH.update(_sb("hb", [128, 32], "float16"))
+SCRATCH.update(_sb("FL SL CL HL S1 S2", [128, 32], "uint16"))
+for _b in range(8):
+    SCRATCH["p%d" % _b] = ("psum", [128, 512], "float32")
+SEMAPHORES = ["sV", "sS", "sT", "sG"] + ["ld%d" % j for j in range(9)] + ["st%d" % j for j in range(8)]
+for _t in range(2):
+    SEMAPHORES += ["as%d" % _t, "ls%d" % _t] + ["%s%d%d" % (n, _t, b) for n in ("ac", "lc") for b in range(len(MV))]
+
+
+def rank_program(g, core, T, topo):
+    rank = T.rank_of(core)
+    if rank is None:
+        return
+    ENG = {"V": g.vector, "S": g.scalar, "T": g.tensor, "G": g, "Y": g.sync}
+    known = {e: {} for e in ENG}
+    cnt, hist = {}, {}
+
+    def bank(n):
+        return n[0] == "p" and n[1:].isdigit()
+
+    def touch(e, rd, wr):
+        toks = []
+        for regs, w in ((rd, 0), (wr, 1)):
+            for (n, a, b) in regs:
+                for (ha, hb, tok, hw, he) in hist.get(n, []):
+                    if he == e and e == "T":
+                        continue
+                    if bank(n):
+                        if he != e or hw or w:
+                            toks.append(tok)
+                    elif ha < b and a < hb and (w or hw):
+                        toks.append(tok)
+        best = {}
+        for tok in toks:
+            if known[e].get(tok[0], 0) < tok[1] and (tok[0] not in best or best[tok[0]][1] < tok[1]):
+                best[tok[0]] = tok
+        todo = [t for t in best.values() if not any(o is not t and o[2].get(t[0], 0) >= t[1] for o in best.values())]
+        for t in todo:
+            ENG[e].wait_ge(T.sem[t[0]], t[1])
+            for s, v in list(t[2].items()) + [(t[0], t[1])]:
+                known[e][s] = max(known[e].get(s, 0), v)
+
+    def note(e, tok, rd, wr):
+        for regs, w in ((rd, 0), (wr, 1)):
+            for (n, a, b) in regs:
+                h = hist.setdefault(n, [])
+                if bank(n):
+                    h[:] = [(0, 512, tok, any(x[3] for x in h if x[4] == e) or w, e)]
+                    continue
+                if w:
+                    h[:] = [x for x in h if not (a <= x[0] and x[1] <= b)]
+                else:
+                    h[:] = [x for x in h if not (x[4] == e and not x[3] and a <= x[0] and x[1] <= b)]
+                h.append((a, b, tok, w, e))
+
+    def op(e, f, rd, wr, sem=None, inc=1):
+        touch(e, rd, wr)
+        s = sem or "s" + e
+        cnt[s] = cnt.get(s, 0) + inc
+        f().then_inc(T.sem[s], inc)
+        note(e if sem is None else sem, (s, cnt[s], dict(known[e])), rd, wr)
+
+    def v(n, a=0, b=None, st=1, p=128):
+        b = T[n].shape[1] if b is None else b
+        return (T[n][0:p, a:b:st] if st > 1 else T[n][0:p, a:b], [(n, a, b)])
+
+    def ind(win, off):
+        return (win[0].indirect(off[0]), win[1] + off[1])
+
+    def tt(o, x, y, f):
+        op("V", lambda: g.vector.tensor_tensor(o[0], x[0], y[0], f), x[1] + y[1], o[1])
+
+    def ts(o, x, s1, f0, s2=None, f1=None):
+        rd = x[1] + (s1[1] if isinstance(s1, tuple) else [])
+        q1 = s1[0] if isinstance(s1, tuple) else s1
+        if f1 is None:
+            op("V", lambda: g.vector.tensor_scalar(o[0], x[0], q1, None, f0), rd, o[1])
+        else:
+            op("V", lambda: g.vector.tensor_scalar(o[0], x[0], q1, s2, f0, f1), rd, o[1])
+
+    def cp(o, x):
+        op("V", lambda: g.vector.tensor_copy(o[0], x[0]), x[1], o[1])
+
+    def fill(o, c):
+        op("V", lambda: g.vector.memset(o[0], c), [], o[1])
+
+    def act(o, x, f, bias=0.0, scale=1.0):
+        rd = x[1] + (bias[1] if isinstance(bias, tuple) else [])
+        bb = bias[0] if isinstance(bias, tuple) else bias
+        op("S", lambda: g.scalar.activation(o[0], x[0], f, bias=bb, scale=scale), rd, o[1])
+
+    def mm(groups):
+        def f():
+            ins = None
+            for o, prs in groups:
+                for j, (l, r) in enumerate(prs):
+                    ins = g.tensor.matmul(o[0], l[0], r[0], j == 0, j == len(prs) - 1)
+            return ins
+        op("T", f, [x for o, prs in groups for l, r in prs for x in l[1] + r[1]], [x for o, prs in groups for x in o[1]])
+
+    def iota(o, pattern, base, ch):
+        op("G", lambda: g.iota(o[0], pattern, base, ch), [], o[1])
+
+    nld = [0, 0]
+
+    def load(o, src, e="Y"):
+        s = "ld%d" % nld[0]
+        nld[0] += 1
+        op(e, lambda: ENG[e].dma_start(o[0], src), [], o[1], s, 16)
+
+    def store(dst, src, e="Y"):
+        s = "st%d" % nld[1]
+        nld[1] += 1
+        op(e, lambda: ENG[e].dma_start(dst, src[0]), src[1], [], s, 16)
+
+    load(v("lst", 0, 512, 1, 8), T.gs[:], "S")
+    load(v("frb"), T.fr[:])
+    load(v("lst", 512, 1024, 1, 8), T.gf[:], "S")
+    load(v("skb"), T.sk[:])
+    load(v("lst", 1024, 1536, 1, 8), T.gcl[:], "S")
+    load(v("xr", 592, 8192), T.x[:, 0:7600])
+    load(v("xr", 0, 592), T.x[:, 7600:8192])
+    load(v("thi"), T.th[:])
+
+    iota(v("it", 0, 128), [[-1, 128]], 0, 1)
+    iota(v("it", 384, 512), [[1, 8], [0, 16]], 0, -1)
+    iota(v("oi"), [[1, 512]], 512, 0)
+    iota(v("it", 128, 256), [[1, 8], [0, 16]], 0, 0)
+    iota(v("it", 256, 384), [[0, 128]], 0, 1)
+    iota(v("il", 0, 16), [[-1, 16]], 16, 1)
+    iota(v("il", 16, 32), [[16, 16]], 15, 0)
+    iota(v("il", 32, 64), [[16, 32]], 16, 0)
+    iota(v("il", 64, 96), [[0, 32]], 0, 1)
+    iota(v("it", 512, 640), [[0, 8], [-1, 16]], 16, 0)
+    ONE = v("Ib", 0, 128)
+
+    def IM(j):
+        return v("Ib", 128 * j, 128 * j + 128)
+    BO, NBO, ONES = v("BO", 0, 128), v("BO", 128, 256), v("BO", 256, 384)
+    R1 = v("row", 256, 384, 1, 1)
+    ts(ONE, v("it", 0, 128), 0, A.is_equal)
+    ts(IM(8), ONE, 2048.0, A.mult)
+    ts(IM(9), ONE, float((1 << 24) + (1 << 21)), A.mult)
+    fill(v("V8", 0, 144, 1, 8), 0.0)
+    cp(v("V8", 15, 143, 16, 8), v("Ib", 0, 8, 1, 8))
+    ts(v("E8", 0, 128, 1, 8), v("it", 384, 512, 1, 8), 0, A.is_equal)
+    ts(v("lo"), v("frb"), 1023, A.bitwise_and)
+    ts(v("p3"), v("frb"), 2.0, A.mult)
+    tt(v("yv"), v("p3"), v("lo"), A.subtract)
+    ts(v("p3"), v("yv"), 0.0, A.is_lt, float(-(1 << 23) - C0 + 1025), A.mult)
+    tt(v("yv"), v("yv"), v("p3"), A.add)
+    ts(v("FB", 0, 512), v("yv"), float(C0), A.add)
+    cp(v("lsh", 0, 1024, 1, 8), v("lst", 0, 1024, 1, 8))
+    mm([(v("p5", 0, 64), [(v("V8", 15 - q, 143 - q, 1, 8), v("lsh", q, 1024, 16, 8)) for q in range(16)])])
+    mm([(v("p4"), [(v("E8", 0, 128, 1, 8), v("lsh", 512, 1024, 1, 8))])])
+    act(v("bR"), v("p4"), F.Copy)
+    for j in range(2):
+        c = (512 * j, 512 * j + 512)
+        q = "p%d" % (6 + j)
+        cp(v("skh", *c), v("skb", *c))
+        ts(v("skv", *c), v("skh", *c), 1024.0, A.is_lt)
+        mm([(v(q), [(IM(8), v("skh", *c)), (IM(9), v("skv", *c))])])
+        act(v("T1", *c), v(q), F.Copy, float(C0 - (1 << 21) - (1 << 22)))
+    cp(v("SL"), v("p5", 0, 32))
+    cp(v("FL"), v("p5", 32, 64))
+
+    def constants_a():
+        cp(v("lsh", 1024, 1536, 1, 8), v("lst", 1024, 1536, 1, 8))
+        mm([(v("p5", 64, 96), [(v("V8", 15 - q, 143 - q, 1, 8), v("lsh", 1024 + q, 1536, 16, 8)) for q in range(16)])])
+        ts(v("CB"), v("oi"), float(-512 - (1 << 23)), A.add)
+        cp(v("CL"), v("p5", 64, 96))
+        for j, c in enumerate((65536.0, 4096.0, float(-(1 << 24)), float(-(1 << 23)), -1.0, float(-3 * (1 << 23)), 1024.0)):
+            ts(IM(j + 1), ONE, c, A.mult)
+        ts(v("it", 256, 384), v("it", 256, 384), 4, A.arith_shift_right)
+        tt(BO, v("it", 128, 256), v("it", 256, 384), A.is_equal)
+        fill(v("Vm"), 0.0)
+        cp(v("Vm", 15, 143, 16), v("BO", 0, 128, 16))
+        ts(v("SF0", 0, 32), v("p5", 0, 32), 592.0, A.add)
+        ts(v("SF0", 32, 64), v("p5", 32, 64), 16.0, A.add)
+        ts(v("CP0"), v("p5", 64, 96), 592.0, A.add)
+
+    def constants_b():
+        cp(v("If"), ONE)
+        ts(v("th2", 0, 1), v("thi"), 4096.5, A.add)
+        ts(v("th2", 1, 2), v("thi"), -0.5, A.add)
+        ts(NBO, BO, -2.0, A.mult)
+        fill(ONES, 1.0)
+        cp(v("Ex"), v("il", 16, 32))
+        fill(v("seg"), 1.0)
+        fill(v("seg", 0, 256, 16), 0.0)
+        cp(v("row", 0, 128), v("it", 512, 640))
+        fill(v("row", 256, 384), 1.0)
+        fill(v("row", 640, 1152), float(1 << 24))
+        fill(v("row", 1152, 1664), float(-(1 << 23)))
+        ts(v("il", 64, 96), v("il", 64, 96), 15, A.bitwise_and)
+        tt(v("IL"), v("il", 64, 96), v("il", 32, 64), A.add)
+
+    def constants_c():
+        cp(v("CI"), v("oi"))
+        ts(v("il", 0, 16), v("il", 0, 16), 15, A.bitwise_and)
+        ts(v("M16"), v("il", 0, 16), 0, A.is_equal)
+        for y in range(16):
+            ts(v("BY", 128 * y, 128 * y + 128), BO, v("M16", y, y + 1), A.mult)
+
+    def Wq(q):
+        return v("Vm", 15 - q, 143 - q)
+
+    def offs(a, e, X, P, Q, O):
+        h = 0 if O == "OG" else 512
+        ts(v(P, a, e), v(X, a, e), 11, A.arith_shift_right, 2047, A.bitwise_and)
+        ts(v(Q, a, e), v(X, a, e), 2047, A.bitwise_and)
+        tt(v("PR", h + a, h + e), v(P, a, e), v(Q, a, e), A.mult)
+        ts(v("OI", h + a, h + e), v("PR", h + a, h + e), 4, A.arith_shift_right, 8191, A.bitwise_and)
+        cp(v(O, a, e), v("OI", h + a, h + e))
+
+    OWN = (0, 512, 1536)
+    SLT = ("SL", "S1", "S2")
+
+    def goal_a(t, a, e):
+        tt(v("AG", a, e), ind(v("T1"), v(SLT[t], a // 16, e // 16)), v("CI", a, e) if t else v("bR", a, e), A.add)
+
+    def goal(t, a, e):
+        goal_a(t, a, e)
+        if t == 0:
+            tt(v("XG", a, e), ind(v("FB", 0, 512), v("FL", a // 16, e // 16)), v("AG", a, e), A.max)
+        else:
+            o = OWN[t] + 512
+            tt(v("XG", a, e), v("FB", o + a, o + e), v("AG", a, e), A.max)
+        offs(a, e, "XG", "PG", "QG", "OG")
+
+    def clause_a(t, a, e):
+        tt(v("AC", a, e), ind(v("T1"), v("CL", a // 16, e // 16)), v("bR", a, e) if t else v("CB", a, e), A.add)
+
+    def clause(t, a, e):
+        if t == 0:
+            clause_a(t, a, e)
+            tt(v("XC", a, e), v("FB", a, e), v("AC", a, e), A.max)
+        else:
+            tt(v("XC", a, e), ind(v("FB", OWN[t], OWN[t] + 1024), v("HL", a // 16, e // 16)), v("AC", a, e), A.max)
+        offs(a, e, "XC", "PC", "QC", "OC")
+        ts(v("nfr", a, e), v("XC", a, e), float(-(1 << 23)), A.not_equal)
+
+    def prep_mm(a, e):
+        mm([(v("p6", a, e), [(IM(3), v("nfr", a, e))])])
+
+    def own_prep(t, a, e):
+        p = v("p6", a, e)
+        ts(v("EG", a, e), v("XG", a, e), (1 << 22) - 1, A.bitwise_and)
+        tt(p, v("EG", a, e), p, A.add)
+        tt(v("cand", a, e), v("FB", OWN[t] + a, OWN[t] + e), p, A.max)
+
+    def grec(j):
+        act(v("U", 2048 * j, 2048 * j + 2048), ind(v("xr"), v("OG", 128 * j, 128 * j + 128)), F.Copy)
+
+    def crec(j, lo=0, n=128):
+        a, e = 128 * j + lo, 128 * j + lo + n
+        tt(v("Df", 16 * a, 16 * e), ind(v("xr"), v("OC", a, e)), v("U", 16 * a, 16 * e), A.subtract)
+
+    def absd(j, lo=0, n=128):
+        a, e = 128 * j + lo, 128 * j + lo + n
+        act(v("Df", 16 * a, 16 * e), v("Df", 16 * a, 16 * e), F.Abs)
+        dsum(a, e)
+
+    def crec_s(j):
+        act(v("Df", 2048 * j, 2048 * j + 2048), ind(v("xr"), v("OC", 128 * j, 128 * j + 128)), F.Copy)
+        for m in range(4):
+            c = (2048 * j + 512 * m, 2048 * j + 512 * m + 512)
+            p = v("p7" if m % 2 else "p1")
+            mm([(p, [(ONE, v("Df", *c)), (IM(5), v("U", *c))])])
+            act(v("Df", *c), p, F.Abs)
+        dsum(128 * j, 128 * j + 128)
+
+    def dbank(a):
+        return "p0" if a < CH[0][1] else "p1" if a < CH[1][1] else "p7"
+
+    def dsum(a, e):
+        mm([(v(dbank(a), a, e), [(Wq(k), v("Df", 16 * a + k, 16 * e, 16)) for k in range(16)] + [(IM(2), v("nfr", a, e))])])
+
+    def keys(t, a, e):
+        D = v(dbank(a), a, e)
+        act(v("sgn", a, e), D, F.Sign, v("th2", 0, 1), -1.0)
+        act(v("Dc", a, e), D, F.Relu, -65536.0, 16.0)
+        mm([(v("p4", a, e), [(BO, v("sgn", a, e))] + ([(ONE, v("a2", a, e))] if t else []))])
+        mm([(v("p2", m, m + 128), [(v("Dc", m, m + 128), v("If")), (R1, v("row", 0, 128, 1, 1)),
+                                   (v("sgn", m, m + 128), IM(1))]) for m in range(a, e, 128)])
+
+    def keys_b(a, e):
+        act(v("kS", a, e), v("p2", a, e), F.Copy)
+        act(v("sc", a, e), v("p4", a, e), F.Sign, 1.0, -1.0)
+        act(v("sg2", a, e), v("Dc", a, e), F.Sign, v("th2", 1, 2), -0.125)
+        mm([(v("p4", a, e), [(IM(4), v("sc", a, e)), (R1, v("row", 1152 + a, 1152 + e, 1, 1))])])
+
+    def best(t, a, e):
+        op("V", lambda: g.vector.tensor_tensor_scan(v("Mx", a, e)[0], v("seg", 0, e - a)[0], v("kS", a, e)[0], 0.0, A.mult, A.max),
+           [("seg", 0, 256), ("kS", a, e)], [("Mx", a, e)])
+        tt(v("oh", a, e), ind(v("Mx", a, e), v("Ex", 0, (e - a) // 16)), v("kS", a, e), A.is_equal)
+        mm([(v("p3", m, m + 128), [(v("oh", m, m + 128), ONE)]) for m in range(a, e, 128)])
+        mm([(v("p2", m, m + 128), [(v("oh", m, m + 128), ONE), (ONE, v("sg2", m, m + 128))]) for m in range(a, e, 128)])
+        act(v("zb", a, e), v("p2", a, e), F.Relu, -1.0)
+
+    def zcol(a, e, j, n):
+        tt(v("Z", 512 * j + a, 512 * j + e), v(n, a, e), v("p3", a, e), A.mult)
+
+    def lsum(p, o, n, a, e):
+        return (v(p, o, o + (e - a) // 16), [(Wq(q), v(n, a + q, e, 16)) for q in range(16)])
+
+    def choose_goal(t, a, e):
+        zcol(a, e, 1, "QG")
+        zcol(a, e, 0, "PG")
+
+    def choose_clause(t, a, e):
+        zcol(a, e, 2, "PC")
+        zcol(a, e, 3, "QC")
+
+    def own_new(t, a, e):
+        p = v("p4", a, e)
+        tt(p, v("cand", a, e), p, A.add)
+        o = v("FB", OWN[t + 1] + a, OWN[t + 1] + e) if t < 2 else v("oi", a, e)
+        tt(o, v("keep", a, e) if t else v("FB", a, e), p, A.max)
+
+    def marks(t, a, e):
+        prs = [(IM(5), v("nfr", a, e)), (NBO, v("zb", a, e)), (IM(5), v("sc", a, e))]
+        if t:
+            prs.append((ONE, v("mu", a, e)))
+        mm([(v("p4", a, e), prs)])
+        act(v("mf" if t == 2 else "mu", a, e), v("p4", a, e), F.Relu)
+
+    def lists_goal(t):
+        c2, d, G2 = v("cl2"), v("dd"), v("p5", 0, 64)
+        ts(v("cl2", 0, 32), v("p5", 128, 160), 0.0, A.is_gt)
+        ts(v("cl2", 32, 64), v("p5", 128, 160), 0.0, A.is_gt)
+        tt(d, v("SF0"), G2, A.subtract)
+        tt(d, d, c2, A.mult)
+        tt(v("SF"), d, G2, A.add)
+        if t < 2:
+            ts(v("SL"), v("SF", 0, 32), -592.0, A.add)
+            ts(v("fxi"), v("SF", 32, 64), 496.0, A.add)
+            ts(v("fxi"), v("fxi"), 1023, A.bitwise_and)
+            cp(v("FL"), v("fxi"))
+
+    def lists_clause(t):
+        d, ch, c2, m = v("cz"), v("CHd"), v("cl2"), v("m1")
+        ts(d, v("p6", 0, 64), 0.0, A.is_equal)
+        tt(d, d, v("p5", 0, 64), A.mult)
+        tt(v("CM"), d, v("p6", 0, 64), A.add)
+        tt(d, v("NXH"), v("CM"), A.subtract)
+        tt(d, d, c2, A.mult)
+        tt(ch, d, v("CM"), A.add)
+        if t < 2:
+            ts(v("CL"), v("CHd", 0, 32), -592.0, A.add)
+            ts(v("hb"), v("CHd", 32, 64), -16.0, A.add)
+            tt(m, v("CHd", 32, 64), v("IL"), A.is_equal)
+            ts(v("eqb"), m, float(-(1 << 23)), A.mult)
+            ts(v("HL"), v("CHd", 32, 64), -16.0, A.add)
+
+    def lists_save():
+        q, c2, m = v("tq"), v("cl2"), v("m1")
+        tt(v("zz"), v("p6", 64, 128), c2, A.is_gt)
+        tt(q, v("SF"), v("SF0"), A.subtract)
+        tt(q, q, v("zz"), A.mult)
+        tt(v("SF0"), v("SF0"), q, A.add)
+        tt(m, v("zz", 0, 32), v("cl2", 0, 32), A.add)
+        tt(v("tq", 0, 32), v("CHd", 0, 32), v("CP0"), A.subtract)
+        tt(m, m, v("tq", 0, 32), A.mult)
+        tt(v("CP0"), v("CP0"), m, A.add)
+
+    def next_clash():
+        n, s, i = v("nx", 0, 32), v("nx", 32, 64), v("nxi")
+        ts(n, v("CP0"), -592.0, A.add)
+        ts(s, v("SF0", 0, 32), -592.0, A.add)
+        tt(i, n, s, A.mult)
+        ts(i, i, 5, A.arith_shift_right)
+        ts(n, n, 1.0, A.add)
+        tt(i, i, n, A.add)
+        ts(i, i, 1023, A.bitwise_and)
+        ts(v("NXH", 0, 32), i, 592.0, A.add)
+        cp(v("NXH", 32, 64), v("IL"))
+
+    def send(t, dst_view, src_view, rs, ls):
+        dst = T.cores[(rank + t + 1) % len(T.cores)]
+        rid, pid, _ = topo.addr(dst)
+        k = len(topo.engines(core, dst))
+        touch("G", src_view[1], [])
+        g.remote_dma(dst_view[0], src_view[0], T.sem[rs], T.sem[ls], pid, rid, topo.mask(core, dst))
+        cnt[ls] = k
+        note(ls, (ls, k, dict(known["G"])), src_view[1], [])
+        src = T.cores[(rank - t - 1) % len(T.cores)]
+        cnt[rs] = len(topo.engines(src, core))
+        note(rs, (rs, cnt[rs], {}), [], dst_view[1])
+
+    def frames_out(a, e):
+        y = v("yv", a, e)
+        ts(v("lo", a, e), v("oi", a, e), 2047, A.bitwise_and)
+        tt(y, v("oi", a, e), v("lo", a, e), A.add)
+        ts(y, y, float(-C0 - 16), A.add, -1.0, A.max)
+        tt(y, y, v("mf", a, e), A.add)
+        store(T.yf[:, a:e], y)
+
+    H0, H1 = (0, 256), (256, 512)
+    for t in range(3):
+        for j in range(2):
+            goal(t, 128 * j, 128 * j + 128)
+            grec(j)
+        if t == 0:
+            constants_a()
+        if t:
+            lists_save()
+            for c in (H0, H1):
+                clause_a(t, *c)
+        clause(t, *H0)
+        prep_mm(*H0)
+        crec_s(0)
+        goal(t, *H1)
+        grec(2)
+        own_prep(t, *H0)
+        clause(t, *H1)
+        prep_mm(*H1)
+        crec(1)
+        absd(1)
+        grec(3)
+        own_prep(t, *H1)
+        if t == 0:
+            constants_b()
+        next_clash()
+        if t:
+            tt(v("keep"), v("FB", OWN[t], OWN[t] + 512), v("p2"), A.min)
+        keys(t, *CH[0])
+        crec(2)
+        absd(2)
+        crec(3, 0, 64)
+        keys_b(*CH[0])
+        crec(3, 64, 64)
+        absd(3, 0, 64)
+        best(t, *CH[0])
+        keys(t, *CH[1])
+        absd(3, 64, 64)
+        choose_goal(t, *CH[0])
+        own_new(t, *CH[0])
+        keys_b(*CH[1])
+        keys(t, *CH[2])
+        best(t, *CH[1])
+        keys_b(*CH[2])
+        choose_goal(t, *CH[1])
+        own_new(t, *CH[1])
+        mm([lsum("p5", 128, "sc", 0, 512)])
+        best(t, *CH[2])
+        choose_goal(t, *CH[2])
+        mm([lsum("p5", 0, "Z", 0, 1024)])
+        own_new(t, *CH[2])
+        lists_goal(t)
+        marks(t, *CH[0])
+        marks(t, *CH[1])
+        if t < 2:
+            send(t, v(SLT[t + 1]), v("SL"), "as%d" % t, "ls%d" % t)
+            first = (0, 1024)[t]
+            o = OWN[t + 1] + 512
+            for b, (a, e) in enumerate(MV):
+                cp(v("col", a, e), ind(v("FB", first, first + 1024), v("FL", a // 16, e // 16)))
+                send(t, v("FB", o + a, o + e), v("col", a, e), "ac%d%d" % (t, b), "lc%d%d" % (t, b))
+        choose_clause(t, 0, 512)
+        if t < 2:
+            mm([(v("p7"), [(ONES, v("sc"))])])
+            ts(v("ai"), v("p7"), 1.0 / 32, A.mult, 4.0, A.add)
+            ts(v("ai"), v("ai"), 1, A.bitwise_and)
+            ts(v("a2"), v("ai"), 2.0, A.mult)
+        mm([lsum("p6", 0, "Z", 1024, 2048)])
+        if t == 0:
+            constants_c()
+        marks(t, *CH[2])
+        if t < 2:
+            mm([(v("p2"), [(R1, v("row", 640, 1152, 1, 1)), (IM(6), v("mu"))])])
+        lists_clause(t)
+        mm([lsum("p6", 64, "zb", 0, 512), lsum("p6", 96, "zb", 0, 512)])
+        if t < 2:
+            mm([(v("p1", y, 512, 16), [(v("BY", 128 * y, 128 * y + 128), v("hb")), (v("BY", 128 * y, 128 * y + 128), v("eqb"))]) for y in range(16)])
+            act(v("bR"), v("p1"), F.Copy)
+        else:
+            lists_save()
+    for j, n in enumerate(("SF", "CHd", "SF0")):
+        ts(v("fo", 32 * j, 32 * j + 32), v(n, 0, 32), -592.0, A.add)
+        ts(v("fi", 32 * j, 32 * j + 32), v(n, 32, 64), -16.0, A.add)
+    ts(v("fi", 96, 128), v("CP0"), -592.0, A.add)
+    ts(v("fo", 96, 128), v("CP0"), 0.0, A.mult)
+    for q in range(4):
+        p = ("p1", "p7", "p5", "p6")[q]
+        mm([(v(p, 128 * y, 128 * y + 128, 1, 8), [(v("Ib", 128 * 7 + q + 4 * y, 1024, 16), v("fo")), (v("Ib", q + 4 * y, 128, 16), v("fi"))]) for y in range(4)])
+    frames_out(*H0)
+    frames_out(*H1)
+    for q in range(4):
+        for y in range(4):
+            o, x = v("OUT", q + 4 * y, 2048, 16, 8), v(("p1", "p7", "p5", "p6")[q], 128 * y, 128 * y + 128, 1, 8)
+            if q == 3:
+                cp(o, x)
+            else:
+                act(o, x, F.Copy)
+    for j, n in enumerate(("yg", "yc", "ysg", "yk")):
+        store(T[n][:], v("OUT", 512 * j, 512 * j + 512, 1, 8), "S" if j % 2 else "Y")
+    for s in cnt:
+        g.wait_ge(T.sem[s], cnt[s])

@@ -8,7 +8,7 @@ def _sb(names, shape, d):
     return {n: ("sbuf", shape, d) for n in names.split()}
 SCRATCH = {"xr": ("sbuf", [128, 8192], "bfloat16"), "T1": ("sbuf", [128, 1024], "float32"), "FB": ("sbuf", [128, 2560], "float32"),
            "PR": ("sbuf", [128, 1024], "int32"), "OI": ("sbuf", [128, 1024], "int32"), "Z": ("sbuf", [128, 2048], "float16"),
-           "Ib": ("sbuf", [128, 1280], "bfloat16"), "BO": ("sbuf", [128, 384], "bfloat16"), "BY": ("sbuf", [128, 2048], "bfloat16"),
+           "Ib": ("sbuf", [128, 1408], "bfloat16"), "BO": ("sbuf", [128, 384], "bfloat16"), "BY": ("sbuf", [128, 2048], "bfloat16"),
            "row": ("sbuf", [128, 1664], "bfloat16"), "it": ("sbuf", [128, 640], "int32"), "il": ("sbuf", [128, 128], "int32"),
            "If": ("sbuf", [128, 128], "float32"), "E8": ("sbuf", [128, 128], "bfloat16"), "seg": ("sbuf", [128, 256], "float32"),
            "thi": ("sbuf", [128, 1], "int32"), "th2": ("sbuf", [128, 8], "float32"), "M16": ("sbuf", [128, 16], "float32"),
@@ -17,7 +17,7 @@ SCRATCH = {"xr": ("sbuf", [128, 8192], "bfloat16"), "T1": ("sbuf", [128, 1024], 
            "OUT": ("sbuf", [128, 2048], "float32"), "fo": ("sbuf", [128, 128], "float16"), "fi": ("sbuf", [128, 128], "float16"),
            "Vm": ("sbuf", [128, 144], "bfloat16"), "V8": ("sbuf", [128, 144], "bfloat16")}
 SCRATCH.update(_sb("U Df", [128, 8192], "bfloat16"))
-SCRATCH.update(_sb("AG AC bR cand keep Dc Mx kS col CI CB yv mf", [128, 512], "float32"))
+SCRATCH.update(_sb("AG AC bR cand keep Dc Mx kS col CI CB yv yr ab", [128, 512], "float32"))
 SCRATCH.update(_sb("XG XC EG PG QG PC QC frb ai oi lo", [128, 512], "int32"))
 SCRATCH.update(_sb("OG OC", [128, 512], "uint16"))
 SCRATCH.update(_sb("nfr mu sgn sg2 sc a2 oh zb", [128, 512], "bfloat16"))
@@ -172,11 +172,10 @@ def rank_program(g, core, T, topo):
     cp(v("V8", 15, 143, 16, 8), v("Ib", 0, 8, 1, 8))
     ts(v("E8", 0, 128, 1, 8), v("it", 384, 512, 1, 8), 0, A.is_equal)
     ts(v("lo"), v("frb"), 1023, A.bitwise_and)
-    ts(v("p3"), v("frb"), 2.0, A.mult)
+    ts(v("p3"), v("frb"), 2.0, A.mult, float(C0), A.add)
     tt(v("yv"), v("p3"), v("lo"), A.subtract)
-    ts(v("p3"), v("yv"), 0.0, A.is_lt, float(-(1 << 23) - C0 + 1025), A.mult)
-    tt(v("yv"), v("yv"), v("p3"), A.add)
-    ts(v("FB", 0, 512), v("yv"), float(C0), A.add)
+    ts(v("p3"), v("yv"), float(C0), A.is_lt, float(-(1 << 23) - C0 + 1025), A.mult)
+    tt(v("FB", 0, 512), v("yv"), v("p3"), A.add)
     cp(v("lsh", 0, 1024, 1, 8), v("lst", 0, 1024, 1, 8))
     mm([(v("p5", 0, 64), [(v("V8", 15 - q, 143 - q, 1, 8), v("lsh", q, 1024, 16, 8)) for q in range(16)])])
     mm([(v("p4"), [(v("E8", 0, 128, 1, 8), v("lsh", 512, 1024, 1, 8))])])
@@ -210,6 +209,10 @@ def rank_program(g, core, T, topo):
         cp(v("If"), ONE)
         ts(v("th2", 0, 1), v("thi"), 4096.5, A.add)
         ts(v("th2", 1, 2), v("thi"), -0.5, A.add)
+        fill(v("th2", 2, 3), -2.0)
+        fill(v("th2", 3, 4), -1.0)
+        fill(v("th2", 4, 5), float(-C0 - 15))
+        ts(IM(10), ONE, -2.0, A.mult)
         ts(NBO, BO, -2.0, A.mult)
         fill(ONES, 1.0)
         cp(v("Ex"), v("il", 16, 32))
@@ -221,6 +224,7 @@ def rank_program(g, core, T, topo):
         fill(v("row", 1152, 1664), float(-(1 << 23)))
         ts(v("il", 64, 96), v("il", 64, 96), 15, A.bitwise_and)
         tt(v("IL"), v("il", 64, 96), v("il", 32, 64), A.add)
+        cp(v("NXH", 32, 64), v("IL"))
 
     def constants_c():
         cp(v("CI"), v("oi"))
@@ -307,14 +311,13 @@ def rank_program(g, core, T, topo):
         D = v(dbank(a), a, e)
         act(v("sgn", a, e), D, F.Sign, v("th2", 0, 1), -1.0)
         act(v("Dc", a, e), D, F.Relu, -65536.0, 16.0)
-        mm([(v("p4", a, e), [(BO, v("sgn", a, e))] + ([(ONE, v("a2", a, e))] if t else []))])
+        mm([(v("p4", a, e), [(BO, v("sgn", a, e))] + ([(IM(10), v("a2", a, e))] if t else []))])
         mm([(v("p2", m, m + 128), [(v("Dc", m, m + 128), v("If")), (R1, v("row", 0, 128, 1, 1)),
                                    (v("sgn", m, m + 128), IM(1))]) for m in range(a, e, 128)])
 
-    def keys_b(a, e):
+    def keys_b(t, a, e):
         act(v("kS", a, e), v("p2", a, e), F.Copy)
-        act(v("sc", a, e), v("p4", a, e), F.Sign, 1.0, -1.0)
-        act(v("sg2", a, e), v("Dc", a, e), F.Sign, v("th2", 1, 2), -0.125)
+        act(v("sc", a, e), v("p4", a, e), F.Sign, -1.0 if t else 1.0, -1.0)
         mm([(v("p4", a, e), [(IM(4), v("sc", a, e)), (R1, v("row", 1152 + a, 1152 + e, 1, 1))])])
 
     def best(t, a, e):
@@ -322,8 +325,11 @@ def rank_program(g, core, T, topo):
            [("seg", 0, 256), ("kS", a, e)], [("Mx", a, e)])
         tt(v("oh", a, e), ind(v("Mx", a, e), v("Ex", 0, (e - a) // 16)), v("kS", a, e), A.is_equal)
         mm([(v("p3", m, m + 128), [(v("oh", m, m + 128), ONE)]) for m in range(a, e, 128)])
-        mm([(v("p2", m, m + 128), [(v("oh", m, m + 128), ONE), (ONE, v("sg2", m, m + 128))]) for m in range(a, e, 128)])
-        act(v("zb", a, e), v("p2", a, e), F.Relu, -1.0)
+
+    def saves():
+        act(v("sg2"), v("Dc"), F.Sign, v("th2", 1, 2), -0.125)
+        mm([(v("p0", m, m + 128), [(v("oh", m, m + 128), ONE), (ONE, v("sg2", m, m + 128))]) for m in range(0, 512, 128)])
+        act(v("zb"), v("p0"), F.Relu, -1.0)
 
     def zcol(a, e, j, n):
         tt(v("Z", 512 * j + a, 512 * j + e), v(n, a, e), v("p3", a, e), A.mult)
@@ -350,7 +356,9 @@ def rank_program(g, core, T, topo):
         if t:
             prs.append((ONE, v("mu", a, e)))
         mm([(v("p4", a, e), prs)])
-        act(v("mf" if t == 2 else "mu", a, e), v("p4", a, e), F.Relu)
+        act(v("p4" if t == 2 else "mu", a, e), v("p4", a, e), F.Relu)
+        if t == 2:
+            act(v("p4", a, e), v("p4", a, e), F.Copy, -1.0)
 
     def lists_goal(t):
         c2, d, G2 = v("cl2"), v("dd"), v("p5", 0, 64)
@@ -381,11 +389,14 @@ def rank_program(g, core, T, topo):
             ts(v("HL"), v("CHd", 32, 64), -16.0, A.add)
 
     def lists_save():
-        q, c2, m = v("tq"), v("cl2"), v("m1")
+        q, c2 = v("tq"), v("cl2")
         tt(v("zz"), v("p6", 64, 128), c2, A.is_gt)
         tt(q, v("SF"), v("SF0"), A.subtract)
         tt(q, q, v("zz"), A.mult)
         tt(v("SF0"), v("SF0"), q, A.add)
+
+    def save_c0():
+        m = v("m1")
         tt(m, v("zz", 0, 32), v("cl2", 0, 32), A.add)
         tt(v("tq", 0, 32), v("CHd", 0, 32), v("CP0"), A.subtract)
         tt(m, m, v("tq", 0, 32), A.mult)
@@ -401,7 +412,6 @@ def rank_program(g, core, T, topo):
         tt(i, i, n, A.add)
         ts(i, i, 1023, A.bitwise_and)
         ts(v("NXH", 0, 32), i, 592.0, A.add)
-        cp(v("NXH", 32, 64), v("IL"))
 
     def send(t, dst_view, src_view, rs, ls):
         dst = T.cores[(rank + t + 1) % len(T.cores)]
@@ -415,13 +425,25 @@ def rank_program(g, core, T, topo):
         cnt[rs] = len(topo.engines(src, core))
         note(rs, (rs, cnt[rs], {}), [], dst_view[1])
 
+    def number_out(j, p, hi, lo):
+        a, b = 32 * j, 32 * j + 32
+        ts(v("fi", a, b), lo, -16.0 if hi else -592.0, A.add)
+        if hi:
+            ts(v("fo", a, b), hi, -592.0, A.add)
+        mm([(v(p, y, 512, 16, 8), [(v("Ib", y, 128, 16), v("fi", a, b))] + ([(v("Ib", 896 + y, 1024, 16), v("fo", a, b))] if hi else []))
+            for y in range(16)])
+        act(v("OUT", 512 * j, 512 * j + 512, 1, 8), v(p, 0, 512, 1, 8), F.Copy)
+        store(T[("yg", "yc", "ysg", "yk")[j]][:], v("OUT", 512 * j, 512 * j + 512, 1, 8))
+
     def frames_out(a, e):
         y = v("yv", a, e)
         ts(v("lo", a, e), v("oi", a, e), 2047, A.bitwise_and)
         tt(y, v("oi", a, e), v("lo", a, e), A.add)
-        ts(y, y, float(-C0 - 16), A.add, -1.0, A.max)
-        tt(y, y, v("mf", a, e), A.add)
-        store(T.yf[:, a:e], y)
+        act(y, y, F.Relu, v("th2", 4, 5))
+
+    def frames_end(a, e):
+        tt(v("yr", a, e), v("yv", a, e), v("p4", a, e), A.add)
+        store(T.yf[:, a:e], v("yr", a, e))
 
     H0, H1 = (0, 256), (256, 512)
     for t in range(3):
@@ -432,6 +454,7 @@ def rank_program(g, core, T, topo):
             constants_a()
         if t:
             lists_save()
+            save_c0()
             for c in (H0, H1):
                 clause_a(t, *c)
         clause(t, *H0)
@@ -455,7 +478,7 @@ def rank_program(g, core, T, topo):
         crec(2)
         absd(2)
         crec(3, 0, 64)
-        keys_b(*CH[0])
+        keys_b(t, *CH[0])
         crec(3, 64, 64)
         absd(3, 0, 64)
         best(t, *CH[0])
@@ -463,20 +486,19 @@ def rank_program(g, core, T, topo):
         absd(3, 64, 64)
         choose_goal(t, *CH[0])
         own_new(t, *CH[0])
-        keys_b(*CH[1])
+        keys_b(t, *CH[1])
         keys(t, *CH[2])
         best(t, *CH[1])
-        keys_b(*CH[2])
+        keys_b(t, *CH[2])
         choose_goal(t, *CH[1])
-        own_new(t, *CH[1])
         mm([lsum("p5", 128, "sc", 0, 512)])
         best(t, *CH[2])
+        own_new(t, *CH[1])
         choose_goal(t, *CH[2])
         mm([lsum("p5", 0, "Z", 0, 1024)])
         own_new(t, *CH[2])
         lists_goal(t)
-        marks(t, *CH[0])
-        marks(t, *CH[1])
+        saves()
         if t < 2:
             send(t, v(SLT[t + 1]), v("SL"), "as%d" % t, "ls%d" % t)
             first = (0, 1024)[t]
@@ -484,43 +506,37 @@ def rank_program(g, core, T, topo):
             for b, (a, e) in enumerate(MV):
                 cp(v("col", a, e), ind(v("FB", first, first + 1024), v("FL", a // 16, e // 16)))
                 send(t, v("FB", o + a, o + e), v("col", a, e), "ac%d%d" % (t, b), "lc%d%d" % (t, b))
+        else:
+            mm([lsum("p6", 64, "zb", 0, 512), lsum("p6", 96, "zb", 0, 512)])
+            number_out(0, "p0", v("SF", 0, 32), v("SF", 32, 64))
         choose_clause(t, 0, 512)
+        if t == 2:
+            lists_save()
+        mm([lsum("p6", 0, "Z", 1024, 2048)])
+        if t == 2:
+            number_out(2, "p1", v("SF0", 0, 32), v("SF0", 32, 64))
         if t < 2:
             mm([(v("p7"), [(ONES, v("sc"))])])
-            ts(v("ai"), v("p7"), 1.0 / 32, A.mult, 4.0, A.add)
-            ts(v("ai"), v("ai"), 1, A.bitwise_and)
-            ts(v("a2"), v("ai"), 2.0, A.mult)
-        mm([lsum("p6", 0, "Z", 1024, 2048)])
+            act(v("ab"), v("p7"), F.Abs, 0.0, 1.0 / 32)
+            act(v("ab"), v("ab"), F.Abs, v("th2", 2, 3))
+            act(v("a2"), v("ab"), F.Abs, v("th2", 3, 4))
         if t == 0:
             constants_c()
-        marks(t, *CH[2])
         if t < 2:
-            mm([(v("p2"), [(R1, v("row", 640, 1152, 1, 1)), (IM(6), v("mu"))])])
+            marks(t, 0, 512)
         lists_clause(t)
-        mm([lsum("p6", 64, "zb", 0, 512), lsum("p6", 96, "zb", 0, 512)])
         if t < 2:
             mm([(v("p1", y, 512, 16), [(v("BY", 128 * y, 128 * y + 128), v("hb")), (v("BY", 128 * y, 128 * y + 128), v("eqb"))]) for y in range(16)])
             act(v("bR"), v("p1"), F.Copy)
-        else:
-            lists_save()
-    for j, n in enumerate(("SF", "CHd", "SF0")):
-        ts(v("fo", 32 * j, 32 * j + 32), v(n, 0, 32), -592.0, A.add)
-        ts(v("fi", 32 * j, 32 * j + 32), v(n, 32, 64), -16.0, A.add)
-    ts(v("fi", 96, 128), v("CP0"), -592.0, A.add)
-    ts(v("fo", 96, 128), v("CP0"), 0.0, A.mult)
-    for q in range(4):
-        p = ("p1", "p7", "p5", "p6")[q]
-        mm([(v(p, 128 * y, 128 * y + 128, 1, 8), [(v("Ib", 128 * 7 + q + 4 * y, 1024, 16), v("fo")), (v("Ib", q + 4 * y, 128, 16), v("fi"))]) for y in range(4)])
+            mm([lsum("p6", 64, "zb", 0, 512), lsum("p6", 96, "zb", 0, 512)])
+            mm([(v("p2"), [(R1, v("row", 640, 1152, 1, 1)), (IM(6), v("mu"))])])
+    number_out(1, "p7", v("CHd", 0, 32), v("CHd", 32, 64))
+    save_c0()
+    number_out(3, "p2", None, v("CP0"))
     frames_out(*H0)
     frames_out(*H1)
-    for q in range(4):
-        for y in range(4):
-            o, x = v("OUT", q + 4 * y, 2048, 16, 8), v(("p1", "p7", "p5", "p6")[q], 128 * y, 128 * y + 128, 1, 8)
-            if q == 3:
-                cp(o, x)
-            else:
-                act(o, x, F.Copy)
-    for j, n in enumerate(("yg", "yc", "ysg", "yk")):
-        store(T[n][:], v("OUT", 512 * j, 512 * j + 512, 1, 8), "S" if j % 2 else "Y")
+    marks(2, 0, 512)
+    frames_end(*H0)
+    frames_end(*H1)
     for s in cnt:
         g.wait_ge(T.sem[s], cnt[s])

@@ -14,7 +14,8 @@ SCRATCH = {"xr": ("sbuf", [128, 8192], "bfloat16"), "T1": ("sbuf", [128, 1024], 
            "thi": ("sbuf", [128, 1], "int32"), "th2": ("sbuf", [128, 8], "float32"), "M16": ("sbuf", [128, 16], "float32"),
            "Ex": ("sbuf", [128, 16], "uint16"), "lst": ("sbuf", [128, 1536], "int32"), "lsh": ("sbuf", [128, 1536], "float16"),
            "skb": ("sbuf", [128, 1024], "int32"), "skh": ("sbuf", [128, 1024], "float16"), "skv": ("sbuf", [128, 1024], "bfloat16"),
-           "OUT": ("sbuf", [128, 2048], "float32"), "fo": ("sbuf", [128, 128], "float16"), "fi": ("sbuf", [128, 128], "float16"),
+           "OUT": ("sbuf", [128, 2048], "float32"), "VmN": ("sbuf", [128, 144], "bfloat16"), "HC0": ("sbuf", [128, 32], "float16"), "HF": ("sbuf", [128, 64], "float16"),
+           "HF0": ("sbuf", [128, 64], "float16"), "HC": ("sbuf", [128, 64], "float16"),
            "Vm": ("sbuf", [128, 144], "bfloat16"), "V8": ("sbuf", [128, 144], "bfloat16")}
 SCRATCH.update(_sb("U Df", [128, 8192], "bfloat16"))
 SCRATCH.update(_sb("AG AC bR cand keep Dc Mx kS col CI CB yv yr ab", [128, 512], "float32"))
@@ -112,9 +113,9 @@ def rank_program(g, core, T, topo):
         op("V", lambda: g.vector.memset(o[0], c), [], o[1])
 
     def act(o, x, f, bias=0.0, scale=1.0):
-        rd = x[1] + (bias[1] if isinstance(bias, tuple) else [])
-        bb = bias[0] if isinstance(bias, tuple) else bias
-        op("S", lambda: g.scalar.activation(o[0], x[0], f, bias=bb, scale=scale), rd, o[1])
+        rd = x[1] + [r for c in (bias, scale) if isinstance(c, tuple) for r in c[1]]
+        bb, cc = [c[0] if isinstance(c, tuple) else c for c in (bias, scale)]
+        op("S", lambda: g.scalar.activation(o[0], x[0], f, bias=bb, scale=cc), rd, o[1])
 
     def mm(groups):
         def f():
@@ -151,10 +152,10 @@ def rank_program(g, core, T, topo):
 
     iota(v("it", 0, 128), [[-1, 128]], 0, 1)
     iota(v("it", 384, 512), [[1, 8], [0, 16]], 0, -1)
-    iota(v("oi"), [[1, 512]], 512, 0)
-    iota(v("it", 128, 256), [[1, 8], [0, 16]], 0, 0)
     iota(v("it", 256, 384), [[0, 128]], 0, 1)
+    iota(v("it", 128, 256), [[1, 8], [0, 16]], 0, 0)
     iota(v("il", 0, 16), [[-1, 16]], 16, 1)
+    iota(v("oi"), [[1, 512]], 512, 0)
     iota(v("il", 16, 32), [[16, 16]], 15, 0)
     iota(v("il", 32, 64), [[16, 32]], 16, 0)
     iota(v("il", 64, 96), [[0, 32]], 0, 1)
@@ -166,20 +167,37 @@ def rank_program(g, core, T, topo):
     BO, NBO, ONES = v("BO", 0, 128), v("BO", 128, 256), v("BO", 256, 384)
     R1 = v("row", 256, 384, 1, 1)
     ts(ONE, v("it", 0, 128), 0, A.is_equal)
-    ts(IM(8), ONE, 2048.0, A.mult)
-    ts(IM(9), ONE, float((1 << 24) + (1 << 21)), A.mult)
     fill(v("V8", 0, 144, 1, 8), 0.0)
     cp(v("V8", 15, 143, 16, 8), v("Ib", 0, 8, 1, 8))
     ts(v("E8", 0, 128, 1, 8), v("it", 384, 512, 1, 8), 0, A.is_equal)
-    ts(v("lo"), v("frb"), 1023, A.bitwise_and)
-    ts(v("p3"), v("frb"), 2.0, A.mult, float(C0), A.add)
-    tt(v("yv"), v("p3"), v("lo"), A.subtract)
-    ts(v("p3"), v("yv"), float(C0), A.is_lt, float(-(1 << 23) - C0 + 1025), A.mult)
-    tt(v("FB", 0, 512), v("yv"), v("p3"), A.add)
+    ts(v("it", 256, 384), v("it", 256, 384), 4, A.arith_shift_right)
+    tt(BO, v("it", 128, 256), v("it", 256, 384), A.is_equal)
+    ts(v("il", 0, 16), v("il", 0, 16), 15, A.bitwise_and)
+    ts(v("M16"), v("il", 0, 16), 0, A.is_equal)
+    fill(v("Vm"), 0.0)
+    cp(v("Vm", 15, 143, 16), v("BO", 0, 128, 16))
+    fill(v("row", 256, 384), 1.0)
+    act(v("VmN"), v("Vm"), F.Copy, 0.0, -1.0)
+    for j, c in ((8, 2048.0), (9, float((1 << 24) + (1 << 21))), (1, 65536.0), (2, 4096.0), (3, float(-(1 << 24))), (4, float(-(1 << 23))),
+                 (5, -1.0), (6, float(-3 * (1 << 23))), (7, 1024.0), (10, -2.0)):
+        act(IM(j), ONE, F.Copy, 0.0, c)
+    act(v("If"), ONE, F.Copy)
+    act(NBO, BO, F.Copy, 0.0, -2.0)
+
+    def by(y):
+        act(v("BY", 128 * y, 128 * y + 128), BO, F.Identity, 0.0, v("M16", y, y + 1))
+    for y in range(8):
+        by(y)
+    cp(v("CI"), v("oi"))
     cp(v("lsh", 0, 1024, 1, 8), v("lst", 0, 1024, 1, 8))
     mm([(v("p5", 0, 64), [(v("V8", 15 - q, 143 - q, 1, 8), v("lsh", q, 1024, 16, 8)) for q in range(16)])])
     mm([(v("p4"), [(v("E8", 0, 128, 1, 8), v("lsh", 512, 1024, 1, 8))])])
     act(v("bR"), v("p4"), F.Copy)
+    act(v("row", 640, 1152), v("bR"), F.Copy, float(1 << 24), 0.0)
+    act(v("row", 1152, 1664), v("bR"), F.Copy, float(-(1 << 23)), 0.0)
+    ts(v("lo"), v("frb"), 1023, A.bitwise_and)
+    ts(v("p3"), v("frb"), 2.0, A.mult, float(C0), A.add)
+    tt(v("yv"), v("p3"), v("lo"), A.subtract)
     for j in range(2):
         c = (512 * j, 512 * j + 512)
         q = "p%d" % (6 + j)
@@ -187,51 +205,39 @@ def rank_program(g, core, T, topo):
         ts(v("skv", *c), v("skh", *c), 1024.0, A.is_lt)
         mm([(v(q), [(IM(8), v("skh", *c)), (IM(9), v("skv", *c))])])
         act(v("T1", *c), v(q), F.Copy, float(C0 - (1 << 21) - (1 << 22)))
+    ts(v("p3"), v("yv"), float(C0), A.is_lt, float(-(1 << 23) - C0 + 1025), A.mult)
+    tt(v("FB", 0, 512), v("yv"), v("p3"), A.add)
     cp(v("SL"), v("p5", 0, 32))
     cp(v("FL"), v("p5", 32, 64))
+    act(v("CB"), v("CI"), F.Copy, float(-512 - (1 << 23)))
+    for y in range(8, 16):
+        by(y)
 
-    def constants_a():
+    def clauses():
         cp(v("lsh", 1024, 1536, 1, 8), v("lst", 1024, 1536, 1, 8))
         mm([(v("p5", 64, 96), [(v("V8", 15 - q, 143 - q, 1, 8), v("lsh", 1024 + q, 1536, 16, 8)) for q in range(16)])])
-        ts(v("CB"), v("oi"), float(-512 - (1 << 23)), A.add)
+
+    def constants_a():
         cp(v("CL"), v("p5", 64, 96))
-        for j, c in enumerate((65536.0, 4096.0, float(-(1 << 24)), float(-(1 << 23)), -1.0, float(-3 * (1 << 23)), 1024.0)):
-            ts(IM(j + 1), ONE, c, A.mult)
-        ts(v("it", 256, 384), v("it", 256, 384), 4, A.arith_shift_right)
-        tt(BO, v("it", 128, 256), v("it", 256, 384), A.is_equal)
-        fill(v("Vm"), 0.0)
-        cp(v("Vm", 15, 143, 16), v("BO", 0, 128, 16))
         ts(v("SF0", 0, 32), v("p5", 0, 32), 592.0, A.add)
         ts(v("SF0", 32, 64), v("p5", 32, 64), 16.0, A.add)
         ts(v("CP0"), v("p5", 64, 96), 592.0, A.add)
 
     def constants_b():
-        cp(v("If"), ONE)
         ts(v("th2", 0, 1), v("thi"), 4096.5, A.add)
         ts(v("th2", 1, 2), v("thi"), -0.5, A.add)
         fill(v("th2", 2, 3), -2.0)
         fill(v("th2", 3, 4), -1.0)
         fill(v("th2", 4, 5), float(-C0 - 15))
-        ts(IM(10), ONE, -2.0, A.mult)
-        ts(NBO, BO, -2.0, A.mult)
         fill(ONES, 1.0)
         cp(v("Ex"), v("il", 16, 32))
         fill(v("seg"), 1.0)
         fill(v("seg", 0, 256, 16), 0.0)
         cp(v("row", 0, 128), v("it", 512, 640))
-        fill(v("row", 256, 384), 1.0)
-        fill(v("row", 640, 1152), float(1 << 24))
-        fill(v("row", 1152, 1664), float(-(1 << 23)))
         ts(v("il", 64, 96), v("il", 64, 96), 15, A.bitwise_and)
         tt(v("IL"), v("il", 64, 96), v("il", 32, 64), A.add)
         cp(v("NXH", 32, 64), v("IL"))
 
-    def constants_c():
-        cp(v("CI"), v("oi"))
-        ts(v("il", 0, 16), v("il", 0, 16), 15, A.bitwise_and)
-        ts(v("M16"), v("il", 0, 16), 0, A.is_equal)
-        for y in range(16):
-            ts(v("BY", 128 * y, 128 * y + 128), BO, v("M16", y, y + 1), A.mult)
 
     def Wq(q):
         return v("Vm", 15 - q, 143 - q)
@@ -301,6 +307,15 @@ def rank_program(g, core, T, topo):
             act(v("Df", *c), p, F.Abs)
         dsum(128 * j, 128 * j + 128)
 
+    def crec_r(j):
+        c = (2048 * j, 2048 * j + 2048)
+        crec(j)
+        ts(v("U", *c), v("Df", *c), 0.0, A.max, 2.0, A.mult)
+        a = 128 * j
+        mm([(v(dbank(a), a, a + 128),
+             [(v("VmN", 15 - k, 143 - k), v("Df", 16 * a + k, 16 * a + 2048, 16)) for k in range(16)]
+             + [(Wq(k), v("U", 16 * a + k, 16 * a + 2048, 16)) for k in range(16)] + [(IM(2), v("nfr", a, a + 128))])])
+
     def dbank(a):
         return "p0" if a < CH[0][1] else "p1" if a < CH[1][1] else "p7"
 
@@ -360,13 +375,15 @@ def rank_program(g, core, T, topo):
         if t == 2:
             act(v("p4", a, e), v("p4", a, e), F.Copy, -1.0)
 
+    LAST = ("S", "S", "H")
+
     def lists_goal(t):
         c2, d, G2 = v("cl2"), v("dd"), v("p5", 0, 64)
         ts(v("cl2", 0, 32), v("p5", 128, 160), 0.0, A.is_gt)
         ts(v("cl2", 32, 64), v("p5", 128, 160), 0.0, A.is_gt)
         tt(d, v("SF0"), G2, A.subtract)
         tt(d, d, c2, A.mult)
-        tt(v("SF"), d, G2, A.add)
+        tt(v(LAST[t] + "F"), d, G2, A.add)
         if t < 2:
             ts(v("SL"), v("SF", 0, 32), -592.0, A.add)
             ts(v("fxi"), v("SF", 32, 64), 496.0, A.add)
@@ -374,7 +391,7 @@ def rank_program(g, core, T, topo):
             cp(v("FL"), v("fxi"))
 
     def lists_clause(t):
-        d, ch, c2, m = v("cz"), v("CHd"), v("cl2"), v("m1")
+        d, ch, c2, m = v("cz"), v("CHd" if t < 2 else "HC"), v("cl2"), v("m1")
         ts(d, v("p6", 0, 64), 0.0, A.is_equal)
         tt(d, d, v("p5", 0, 64), A.mult)
         tt(v("CM"), d, v("p6", 0, 64), A.add)
@@ -388,19 +405,19 @@ def rank_program(g, core, T, topo):
             ts(v("eqb"), m, float(-(1 << 23)), A.mult)
             ts(v("HL"), v("CHd", 32, 64), -16.0, A.add)
 
-    def lists_save():
+    def lists_save(t):
         q, c2 = v("tq"), v("cl2")
         tt(v("zz"), v("p6", 64, 128), c2, A.is_gt)
-        tt(q, v("SF"), v("SF0"), A.subtract)
+        tt(q, v(LAST[t] + "F"), v("SF0"), A.subtract)
         tt(q, q, v("zz"), A.mult)
-        tt(v("SF0"), v("SF0"), q, A.add)
+        tt(v(LAST[t] + "F0"), v("SF0"), q, A.add)
 
-    def save_c0():
+    def save_c0(t):
         m = v("m1")
         tt(m, v("zz", 0, 32), v("cl2", 0, 32), A.add)
-        tt(v("tq", 0, 32), v("CHd", 0, 32), v("CP0"), A.subtract)
+        tt(v("tq", 0, 32), v("CHd" if t < 2 else "HC", 0, 32), v("CP0"), A.subtract)
         tt(m, m, v("tq", 0, 32), A.mult)
-        tt(v("CP0"), v("CP0"), m, A.add)
+        tt(v("CP0" if t < 2 else "HC0"), v("CP0"), m, A.add)
 
     def next_clash():
         n, s, i = v("nx", 0, 32), v("nx", 32, 64), v("nxi")
@@ -426,13 +443,9 @@ def rank_program(g, core, T, topo):
         note(rs, (rs, cnt[rs], {}), [], dst_view[1])
 
     def number_out(j, p, hi, lo):
-        a, b = 32 * j, 32 * j + 32
-        ts(v("fi", a, b), lo, -16.0 if hi else -592.0, A.add)
-        if hi:
-            ts(v("fo", a, b), hi, -592.0, A.add)
-        mm([(v(p, y, 512, 16, 8), [(v("Ib", y, 128, 16), v("fi", a, b))] + ([(v("Ib", 896 + y, 1024, 16), v("fo", a, b))] if hi else []))
+        mm([(v(p, y, 512, 16, 8), [(v("Ib", y, 128, 16), lo)] + ([(v("Ib", 896 + y, 1024, 16), hi)] if hi else []))
             for y in range(16)])
-        act(v("OUT", 512 * j, 512 * j + 512, 1, 8), v(p, 0, 512, 1, 8), F.Copy)
+        act(v("OUT", 512 * j, 512 * j + 512, 1, 8), v(p, 0, 512, 1, 8), F.Copy, float(-592 * 1024 - 16) if hi else -592.0)
         store(T[("yg", "yc", "ysg", "yk")[j]][:], v("OUT", 512 * j, 512 * j + 512, 1, 8))
 
     def frames_out(a, e):
@@ -450,11 +463,13 @@ def rank_program(g, core, T, topo):
         for j in range(2):
             goal(t, 128 * j, 128 * j + 128)
             grec(j)
+            if t + j == 0:
+                clauses()
         if t == 0:
             constants_a()
         if t:
-            lists_save()
-            save_c0()
+            lists_save(t - 1)
+            save_c0(t - 1)
             for c in (H0, H1):
                 clause_a(t, *c)
         clause(t, *H0)
@@ -465,15 +480,10 @@ def rank_program(g, core, T, topo):
         own_prep(t, *H0)
         clause(t, *H1)
         prep_mm(*H1)
-        crec(1)
-        absd(1)
+        crec_r(1)
         grec(3)
-        own_prep(t, *H1)
         if t == 0:
             constants_b()
-        next_clash()
-        if t:
-            tt(v("keep"), v("FB", OWN[t], OWN[t] + 512), v("p2"), A.min)
         keys(t, *CH[0])
         crec(2)
         absd(2)
@@ -481,17 +491,23 @@ def rank_program(g, core, T, topo):
         keys_b(t, *CH[0])
         crec(3, 64, 64)
         absd(3, 0, 64)
+        if t:
+            tt(v("keep"), v("FB", OWN[t], OWN[t] + 512), v("p3"), A.min)
         best(t, *CH[0])
         keys(t, *CH[1])
         absd(3, 64, 64)
+        own_prep(t, *H1)
         choose_goal(t, *CH[0])
         own_new(t, *CH[0])
         keys_b(t, *CH[1])
         keys(t, *CH[2])
         best(t, *CH[1])
+        next_clash()
         keys_b(t, *CH[2])
         choose_goal(t, *CH[1])
         mm([lsum("p5", 128, "sc", 0, 512)])
+        if t == 2:
+            frames_out(*CH[0])
         best(t, *CH[2])
         own_new(t, *CH[1])
         choose_goal(t, *CH[2])
@@ -507,35 +523,31 @@ def rank_program(g, core, T, topo):
                 cp(v("col", a, e), ind(v("FB", first, first + 1024), v("FL", a // 16, e // 16)))
                 send(t, v("FB", o + a, o + e), v("col", a, e), "ac%d%d" % (t, b), "lc%d%d" % (t, b))
         else:
-            mm([lsum("p6", 64, "zb", 0, 512), lsum("p6", 96, "zb", 0, 512)])
-            number_out(0, "p0", v("SF", 0, 32), v("SF", 32, 64))
+            number_out(0, "p1", v("HF", 0, 32), v("HF", 32, 64))
         choose_clause(t, 0, 512)
-        if t == 2:
-            lists_save()
         mm([lsum("p6", 0, "Z", 1024, 2048)])
-        if t == 2:
-            number_out(2, "p1", v("SF0", 0, 32), v("SF0", 32, 64))
         if t < 2:
             mm([(v("p7"), [(ONES, v("sc"))])])
             act(v("ab"), v("p7"), F.Abs, 0.0, 1.0 / 32)
             act(v("ab"), v("ab"), F.Abs, v("th2", 2, 3))
             act(v("a2"), v("ab"), F.Abs, v("th2", 3, 4))
-        if t == 0:
-            constants_c()
         if t < 2:
             marks(t, 0, 512)
+        else:
+            frames_out(*H1)
         lists_clause(t)
         if t < 2:
             mm([(v("p1", y, 512, 16), [(v("BY", 128 * y, 128 * y + 128), v("hb")), (v("BY", 128 * y, 128 * y + 128), v("eqb"))]) for y in range(16)])
             act(v("bR"), v("p1"), F.Copy)
             mm([lsum("p6", 64, "zb", 0, 512), lsum("p6", 96, "zb", 0, 512)])
-            mm([(v("p2"), [(R1, v("row", 640, 1152, 1, 1)), (IM(6), v("mu"))])])
-    number_out(1, "p7", v("CHd", 0, 32), v("CHd", 32, 64))
-    save_c0()
-    number_out(3, "p2", None, v("CP0"))
-    frames_out(*H0)
-    frames_out(*H1)
+            mm([(v("p3"), [(R1, v("row", 640, 1152, 1, 1)), (IM(6), v("mu"))])])
+    mm([lsum("p6", 64, "zb", 0, 512), lsum("p6", 96, "zb", 0, 512)])
+    number_out(1, "p7", v("HC", 0, 32), v("HC", 32, 64))
     marks(2, 0, 512)
+    lists_save(2)
+    save_c0(2)
+    number_out(2, "p1", v("HF0", 0, 32), v("HF0", 32, 64))
+    number_out(3, "p2", None, v("HC0"))
     frames_end(*H0)
     frames_end(*H1)
     for s in cnt:

from concourse.mybir import AluOpType, ActivationFunctionType
A = AluOpType
F = ActivationFunctionType
C0 = 592 * 2048 + 16
CH = ((0, 256), (256, 384), (384, 512))
MV = ((0, 256), (256, 512))
def _sb(names, shape, d):
    return {n: ("sbuf", shape, d) for n in names.split()}
SCRATCH = {"xr": ("sbuf", [128, 8192], "bfloat16"), "T1": ("sbuf", [128, 1024], "float32"), "FB": ("sbuf", [128, 2560], "float32"),
           "PR": ("sbuf", [128, 1024], "int32"), "OI": ("sbuf", [128, 1024], "int32"), "Z": ("sbuf", [128, 2048], "float16"),
           "Ib": ("sbuf", [128, 1408], "bfloat16"), "BO": ("sbuf", [128, 384], "bfloat16"), "BY": ("sbuf", [128, 2048], "bfloat16"),
           "row": ("sbuf", [128, 1664], "bfloat16"), "it": ("sbuf", [128, 640], "int32"), "il": ("sbuf", [128, 128], "int32"),
           "If": ("sbuf", [128, 128], "float32"), "E8": ("sbuf", [128, 128], "bfloat16"), "seg": ("sbuf", [128, 256], "float32"),
           "thi": ("sbuf", [128, 1], "int32"), "th2": ("sbuf", [128, 8], "float32"), "M16": ("sbuf", [128, 16], "float32"),
           "Ex": ("sbuf", [128, 16], "uint16"), "lst": ("sbuf", [128, 1536], "int32"), "lsh": ("sbuf", [128, 1536], "float16"),
           "skb": ("sbuf", [128, 1024], "int32"), "skh": ("sbuf", [128, 1024], "float16"), "skv": ("sbuf", [128, 1024], "bfloat16"),
           "OUT": ("sbuf", [128, 2048], "float32"), "VmN": ("sbuf", [128, 144], "bfloat16"), "HC0": ("sbuf", [128, 32], "float16"), "HF": ("sbuf", [128, 64], "float16"),
           "HF0": ("sbuf", [128, 64], "float16"), "HC": ("sbuf", [128, 64], "float16"),
           "Vm": ("sbuf", [128, 144], "bfloat16"), "V8": ("sbuf", [128, 144], "bfloat16")}
SCRATCH.update(_sb("U Df", [128, 8192], "bfloat16"))
SCRATCH.update(_sb("AG AC bR cand keep Dc Mx kS col CI CB yv yr ab", [128, 512], "float32"))
SCRATCH.update(_sb("XG XC EG PG QG PC QC frb ai oi lo", [128, 512], "int32"))
SCRATCH.update(_sb("OG OC", [128, 512], "uint16"))
SCRATCH.update(_sb("nfr mu sgn sg2 sc a2 oh zb", [128, 512], "bfloat16"))
SCRATCH.update(_sb("SF0 NXH cl2 dd SF cz CM CHd zz tq nx", [128, 64], "float32"))
SCRATCH.update(_sb("IL CP0 m1", [128, 32], "float32"))
SCRATCH.update(_sb("nxi fxi", [128, 32], "int32"))
SCRATCH.update(_sb("eqb", [128, 32], "bfloat16"))
SCRATCH.update(_sb("hb", [128, 32], "float16"))
SCRATCH.update(_sb("FL SL CL HL S1 S2", [128, 32], "uint16"))
for _b in range(8):
    SCRATCH["p%d" % _b] = ("psum", [128, 512], "float32")
SEMAPHORES = ["sV", "sS", "sT", "sG"] + ["ld%d" % j for j in range(9)] + ["st%d" % j for j in range(8)]
for _t in range(2):
    SEMAPHORES += ["as%d" % _t, "ls%d" % _t] + ["%s%d%d" % (n, _t, b) for n in ("ac", "lc") for b in range(len(MV))]


def rank_program(g, core, T, topo):
    rank = T.rank_of(core)
    if rank is None:
        return
    ENG = {"V": g.vector, "S": g.scalar, "T": g.tensor, "G": g, "Y": g.sync}
    known = {e: {} for e in ENG}
    cnt, hist = {}, {}

    def bank(n):
        return n[0] == "p" and n[1:].isdigit()

    def touch(e, rd, wr):
        toks = []
        for regs, w in ((rd, 0), (wr, 1)):
            for (n, a, b) in regs:
                for (ha, hb, tok, hw, he) in hist.get(n, []):
                    if he == e and e == "T":
                        continue
                    if bank(n):
                        if he != e or hw or w:
                            toks.append(tok)
                    elif ha < b and a < hb and (w or hw):
                        toks.append(tok)
        best = {}
        for tok in toks:
            if known[e].get(tok[0], 0) < tok[1] and (tok[0] not in best or best[tok[0]][1] < tok[1]):
                best[tok[0]] = tok
        todo = [t for t in best.values() if not any(o is not t and o[2].get(t[0], 0) >= t[1] for o in best.values())]
        for t in todo:
            ENG[e].wait_ge(T.sem[t[0]], t[1])
            for s, v in list(t[2].items()) + [(t[0], t[1])]:
                known[e][s] = max(known[e].get(s, 0), v)

    def note(e, tok, rd, wr):
        for regs, w in ((rd, 0), (wr, 1)):
            for (n, a, b) in regs:
                h = hist.setdefault(n, [])
                if bank(n):
                    h[:] = [(0, 512, tok, any(x[3] for x in h if x[4] == e) or w, e)]
                    continue
                if w:
                    h[:] = [x for x in h if not (a <= x[0] and x[1] <= b)]
                else:
                    h[:] = [x for x in h if not (x[4] == e and not x[3] and a <= x[0] and x[1] <= b)]
                h.append((a, b, tok, w, e))

    def op(e, f, rd, wr, sem=None, inc=1):
        touch(e, rd, wr)
        s = sem or "s" + e
        cnt[s] = cnt.get(s, 0) + inc
        f().then_inc(T.sem[s], inc)
        note(e if sem is None else sem, (s, cnt[s], dict(known[e])), rd, wr)

    def v(n, a=0, b=None, st=1, p=128):
        b = T[n].shape[1] if b is None else b
        return (T[n][0:p, a:b:st] if st > 1 else T[n][0:p, a:b], [(n, a, b)])

    def ind(win, off):
        return (win[0].indirect(off[0]), win[1] + off[1])

    def tt(o, x, y, f):
        op("V", lambda: g.vector.tensor_tensor(o[0], x[0], y[0], f), x[1] + y[1], o[1])

    def ts(o, x, s1, f0, s2=None, f1=None):
        rd = x[1] + (s1[1] if isinstance(s1, tuple) else [])
        q1 = s1[0] if isinstance(s1, tuple) else s1
        if f1 is None:
            op("V", lambda: g.vector.tensor_scalar(o[0], x[0], q1, None, f0), rd, o[1])
        else:
            op("V", lambda: g.vector.tensor_scalar(o[0], x[0], q1, s2, f0, f1), rd, o[1])

    def cp(o, x):
        op("V", lambda: g.vector.tensor_copy(o[0], x[0]), x[1], o[1])

    def fill(o, c):
        op("V", lambda: g.vector.memset(o[0], c), [], o[1])

    def act(o, x, f, bias=0.0, scale=1.0):
        rd = x[1] + [r for c in (bias, scale) if isinstance(c, tuple) for r in c[1]]
        bb, cc = [c[0] if isinstance(c, tuple) else c for c in (bias, scale)]
        op("S", lambda: g.scalar.activation(o[0], x[0], f, bias=bb, scale=cc), rd, o[1])

    def mm(groups):
        def f():
            ins = None
            for o, prs in groups:
                for j, (l, r) in enumerate(prs):
                    ins = g.tensor.matmul(o[0], l[0], r[0], j == 0, j == len(prs) - 1)
            return ins
        op("T", f, [x for o, prs in groups for l, r in prs for x in l[1] + r[1]], [x for o, prs in groups for x in o[1]])

    def iota(o, pattern, base, ch):
        op("G", lambda: g.iota(o[0], pattern, base, ch), [], o[1])

    nld = [0, 0]

    def load(o, src, e="Y"):
        s = "ld%d" % nld[0]
        nld[0] += 1
        op(e, lambda: ENG[e].dma_start(o[0], src), [], o[1], s, 16)

    def store(dst, src, e="Y"):
        s = "st%d" % nld[1]
        nld[1] += 1
        op(e, lambda: ENG[e].dma_start(dst, src[0]), src[1], [], s, 16)

    load(v("lst", 0, 512, 1, 8), T.gs[:], "S")
    load(v("frb"), T.fr[:])
    load(v("lst", 512, 1024, 1, 8), T.gf[:], "S")
    load(v("skb"), T.sk[:])
    load(v("lst", 1024, 1536, 1, 8), T.gcl[:], "S")
    load(v("xr", 592, 8192), T.x[:, 0:7600])
    load(v("xr", 0, 592), T.x[:, 7600:8192])
    load(v("thi"), T.th[:])

    iota(v("it", 0, 128), [[-1, 128]], 0, 1)
    iota(v("it", 384, 512), [[1, 8], [0, 16]], 0, -1)
    iota(v("it", 256, 384), [[0, 128]], 0, 1)
    iota(v("it", 128, 256), [[1, 8], [0, 16]], 0, 0)
    iota(v("il", 0, 16), [[-1, 16]], 16, 1)
    iota(v("oi"), [[1, 512]], 512, 0)
    iota(v("il", 16, 32), [[16, 16]], 15, 0)
    iota(v("il", 32, 64), [[16, 32]], 16, 0)
    iota(v("il", 64, 96), [[0, 32]], 0, 1)
    iota(v("it", 512, 640), [[0, 8], [-1, 16]], 16, 0)
    ONE = v("Ib", 0, 128)

    def IM(j):
        return v("Ib", 128 * j, 128 * j + 128)
    BO, NBO, ONES = v("BO", 0, 128), v("BO", 128, 256), v("BO", 256, 384)
    R1 = v("row", 256, 384, 1, 1)
    ts(ONE, v("it", 0, 128), 0, A.is_equal)
    fill(v("V8", 0, 144, 1, 8), 0.0)
    cp(v("V8", 15, 143, 16, 8), v("Ib", 0, 8, 1, 8))
    ts(v("E8", 0, 128, 1, 8), v("it", 384, 512, 1, 8), 0, A.is_equal)
    ts(v("it", 256, 384), v("it", 256, 384), 4, A.arith_shift_right)
    tt(BO, v("it", 128, 256), v("it", 256, 384), A.is_equal)
    ts(v("il", 0, 16), v("il", 0, 16), 15, A.bitwise_and)
    ts(v("M16"), v("il", 0, 16), 0, A.is_equal)
    fill(v("Vm"), 0.0)
    cp(v("Vm", 15, 143, 16), v("BO", 0, 128, 16))
    fill(v("row", 256, 384), 1.0)
    act(v("VmN"), v("Vm"), F.Copy, 0.0, -1.0)
    for j, c in ((8, 2048.0), (9, float((1 << 24) + (1 << 21))), (1, 65536.0), (2, 4096.0), (3, float(-(1 << 24))), (4, float(-(1 << 23))),
                 (5, -1.0), (6, float(-3 * (1 << 23))), (7, 1024.0), (10, -2.0)):
        act(IM(j), ONE, F.Copy, 0.0, c)
    act(v("If"), ONE, F.Copy)
    act(NBO, BO, F.Copy, 0.0, -2.0)

    def by(y):
        act(v("BY", 128 * y, 128 * y + 128), BO, F.Identity, 0.0, v("M16", y, y + 1))
    for y in range(8):
        by(y)
    cp(v("CI"), v("oi"))
    cp(v("lsh", 0, 1024, 1, 8), v("lst", 0, 1024, 1, 8))
    mm([(v("p5", 0, 64), [(v("V8", 15 - q, 143 - q, 1, 8), v("lsh", q, 1024, 16, 8)) for q in range(16)])])
    mm([(v("p4"), [(v("E8", 0, 128, 1, 8), v("lsh", 512, 1024, 1, 8))])])
    act(v("bR"), v("p4"), F.Copy)
    act(v("row", 640, 1152), v("bR"), F.Copy, float(1 << 24), 0.0)
    act(v("row", 1152, 1664), v("bR"), F.Copy, float(-(1 << 23)), 0.0)
    ts(v("lo"), v("frb"), 1023, A.bitwise_and)
    ts(v("p3"), v("frb"), 2.0, A.mult, float(C0), A.add)
    tt(v("yv"), v("p3"), v("lo"), A.subtract)
    for j in range(2):
        c = (512 * j, 512 * j + 512)
        q = "p%d" % (6 + j)
        cp(v("skh", *c), v("skb", *c))
        ts(v("skv", *c), v("skh", *c), 1024.0, A.is_lt)
        mm([(v(q), [(IM(8), v("skh", *c)), (IM(9), v("skv", *c))])])
        act(v("T1", *c), v(q), F.Copy, float(C0 - (1 << 21) - (1 << 22)))
    ts(v("p3"), v("yv"), float(C0), A.is_lt, float(-(1 << 23) - C0 + 1025), A.mult)
    tt(v("FB", 0, 512), v("yv"), v("p3"), A.add)
    cp(v("SL"), v("p5", 0, 32))
    cp(v("FL"), v("p5", 32, 64))
    act(v("CB"), v("CI"), F.Copy, float(-512 - (1 << 23)))
    for y in range(8, 16):
        by(y)

    def clauses():
        cp(v("lsh", 1024, 1536, 1, 8), v("lst", 1024, 1536, 1, 8))
        mm([(v("p5", 64, 96), [(v("V8", 15 - q, 143 - q, 1, 8), v("lsh", 1024 + q, 1536, 16, 8)) for q in range(16)])])

    def constants_a():
        cp(v("CL"), v("p5", 64, 96))
        ts(v("SF0", 0, 32), v("p5", 0, 32), 592.0, A.add)
        ts(v("SF0", 32, 64), v("p5", 32, 64), 16.0, A.add)
        ts(v("CP0"), v("p5", 64, 96), 592.0, A.add)

    def constants_b():
        ts(v("th2", 0, 1), v("thi"), 4096.5, A.add)
        ts(v("th2", 1, 2), v("thi"), -0.5, A.add)
        fill(v("th2", 2, 3), -2.0)
        fill(v("th2", 3, 4), -1.0)
        fill(v("th2", 4, 5), float(-C0 - 15))
        fill(ONES, 1.0)
        cp(v("Ex"), v("il", 16, 32))
        fill(v("seg"), 1.0)
        fill(v("seg", 0, 256, 16), 0.0)
        cp(v("row", 0, 128), v("it", 512, 640))
        ts(v("il", 64, 96), v("il", 64, 96), 15, A.bitwise_and)
        tt(v("IL"), v("il", 64, 96), v("il", 32, 64), A.add)
        cp(v("NXH", 32, 64), v("IL"))


    def Wq(q):
        return v("Vm", 15 - q, 143 - q)

    def offs(a, e, X, P, Q, O):
        h = 0 if O == "OG" else 512
        ts(v(P, a, e), v(X, a, e), 11, A.arith_shift_right, 2047, A.bitwise_and)
        ts(v(Q, a, e), v(X, a, e), 2047, A.bitwise_and)
        tt(v("PR", h + a, h + e), v(P, a, e), v(Q, a, e), A.mult)
        ts(v("OI", h + a, h + e), v("PR", h + a, h + e), 4, A.arith_shift_right, 8191, A.bitwise_and)
        cp(v(O, a, e), v("OI", h + a, h + e))

    OWN = (0, 512, 1536)
    SLT = ("SL", "S1", "S2")

    def goal_a(t, a, e):
        tt(v("AG", a, e), ind(v("T1"), v(SLT[t], a // 16, e // 16)), v("CI", a, e) if t else v("bR", a, e), A.add)

    def goal(t, a, e):
        goal_a(t, a, e)
        if t == 0:
            tt(v("XG", a, e), ind(v("FB", 0, 512), v("FL", a // 16, e // 16)), v("AG", a, e), A.max)
        else:
            o = OWN[t] + 512
            tt(v("XG", a, e), v("FB", o + a, o + e), v("AG", a, e), A.max)
        offs(a, e, "XG", "PG", "QG", "OG")

    def clause_a(t, a, e):
        tt(v("AC", a, e), ind(v("T1"), v("CL", a // 16, e // 16)), v("bR", a, e) if t else v("CB", a, e), A.add)

    def clause(t, a, e):
        if t == 0:
            clause_a(t, a, e)
            tt(v("XC", a, e), v("FB", a, e), v("AC", a, e), A.max)
        else:
            tt(v("XC", a, e), ind(v("FB", OWN[t], OWN[t] + 1024), v("HL", a // 16, e // 16)), v("AC", a, e), A.max)
        offs(a, e, "XC", "PC", "QC", "OC")
        ts(v("nfr", a, e), v("XC", a, e), float(-(1 << 23)), A.not_equal)

    def prep_mm(a, e):
        mm([(v("p6", a, e), [(IM(3), v("nfr", a, e))])])

    def own_prep(t, a, e):
        p = v("p6", a, e)
        ts(v("EG", a, e), v("XG", a, e), (1 << 22) - 1, A.bitwise_and)
        tt(p, v("EG", a, e), p, A.add)
        tt(v("cand", a, e), v("FB", OWN[t] + a, OWN[t] + e), p, A.max)

    def grec(j):
        act(v("U", 2048 * j, 2048 * j + 2048), ind(v("xr"), v("OG", 128 * j, 128 * j + 128)), F.Copy)

    def crec(j, lo=0, n=128):
        a, e = 128 * j + lo, 128 * j + lo + n
        tt(v("Df", 16 * a, 16 * e), ind(v("xr"), v("OC", a, e)), v("U", 16 * a, 16 * e), A.subtract)

    def absd(j, lo=0, n=128):
        a, e = 128 * j + lo, 128 * j + lo + n
        act(v("Df", 16 * a, 16 * e), v("Df", 16 * a, 16 * e), F.Abs)
        dsum(a, e)

    def crec_s(j):
        act(v("Df", 2048 * j, 2048 * j + 2048), ind(v("xr"), v("OC", 128 * j, 128 * j + 128)), F.Copy)
        for m in range(4):
            c = (2048 * j + 512 * m, 2048 * j + 512 * m + 512)
            p = v("p7" if m % 2 else "p1")
            mm([(p, [(ONE, v("Df", *c)), (IM(5), v("U", *c))])])
            act(v("Df", *c), p, F.Abs)
        dsum(128 * j, 128 * j + 128)

    def crec_r(j):
        c = (2048 * j, 2048 * j + 2048)
        crec(j)
        ts(v("U", *c), v("Df", *c), 0.0, A.max, 2.0, A.mult)
        a = 128 * j
        mm([(v(dbank(a), a, a + 128),
             [(v("VmN", 15 - k, 143 - k), v("Df", 16 * a + k, 16 * a + 2048, 16)) for k in range(16)]
             + [(Wq(k), v("U", 16 * a + k, 16 * a + 2048, 16)) for k in range(16)] + [(IM(2), v("nfr", a, a + 128))])])

    def dbank(a):
        return "p0" if a < CH[0][1] else "p1" if a < CH[1][1] else "p7"

    def dsum(a, e):
        mm([(v(dbank(a), a, e), [(Wq(k), v("Df", 16 * a + k, 16 * e, 16)) for k in range(16)] + [(IM(2), v("nfr", a, e))])])

    def keys(t, a, e):
        D = v(dbank(a), a, e)
        act(v("sgn", a, e), D, F.Sign, v("th2", 0, 1), -1.0)
        act(v("Dc", a, e), D, F.Relu, -65536.0, 16.0)
        mm([(v("p4", a, e), [(BO, v("sgn", a, e))] + ([(IM(10), v("a2", a, e))] if t else []))])
        mm([(v("p2", m, m + 128), [(v("Dc", m, m + 128), v("If")), (R1, v("row", 0, 128, 1, 1)),
                                   (v("sgn", m, m + 128), IM(1))]) for m in range(a, e, 128)])

    def keys_b(t, a, e):
        act(v("kS", a, e), v("p2", a, e), F.Copy)
        act(v("sc", a, e), v("p4", a, e), F.Sign, -1.0 if t else 1.0, -1.0)
        mm([(v("p4", a, e), [(IM(4), v("sc", a, e)), (R1, v("row", 1152 + a, 1152 + e, 1, 1))])])

    def best(t, a, e):
        op("V", lambda: g.vector.tensor_tensor_scan(v("Mx", a, e)[0], v("seg", 0, e - a)[0], v("kS", a, e)[0], 0.0, A.mult, A.max),
           [("seg", 0, 256), ("kS", a, e)], [("Mx", a, e)])
        tt(v("oh", a, e), ind(v("Mx", a, e), v("Ex", 0, (e - a) // 16)), v("kS", a, e), A.is_equal)
        mm([(v("p3", m, m + 128), [(v("oh", m, m + 128), ONE)]) for m in range(a, e, 128)])

    def saves():
        act(v("sg2"), v("Dc"), F.Sign, v("th2", 1, 2), -0.125)
        mm([(v("p0", m, m + 128), [(v("oh", m, m + 128), ONE), (ONE, v("sg2", m, m + 128))]) for m in range(0, 512, 128)])
        act(v("zb"), v("p0"), F.Relu, -1.0)

    def zcol(a, e, j, n):
        tt(v("Z", 512 * j + a, 512 * j + e), v(n, a, e), v("p3", a, e), A.mult)

    def lsum(p, o, n, a, e):
        return (v(p, o, o + (e - a) // 16), [(Wq(q), v(n, a + q, e, 16)) for q in range(16)])

    def choose_goal(t, a, e):
        zcol(a, e, 1, "QG")
        zcol(a, e, 0, "PG")

    def choose_clause(t, a, e):
        zcol(a, e, 2, "PC")
        zcol(a, e, 3, "QC")

    def own_new(t, a, e):
        p = v("p4", a, e)
        tt(p, v("cand", a, e), p, A.add)
        o = v("FB", OWN[t + 1] + a, OWN[t + 1] + e) if t < 2 else v("oi", a, e)
        tt(o, v("keep", a, e) if t else v("FB", a, e), p, A.max)

    def marks(t, a, e):
        prs = [(IM(5), v("nfr", a, e)), (NBO, v("zb", a, e)), (IM(5), v("sc", a, e))]
        if t:
            prs.append((ONE, v("mu", a, e)))
        mm([(v("p4", a, e), prs)])
        act(v("p4" if t == 2 else "mu", a, e), v("p4", a, e), F.Relu)
        if t == 2:
            act(v("p4", a, e), v("p4", a, e), F.Copy, -1.0)

    LAST = ("S", "S", "H")

    def lists_goal(t):
        c2, d, G2 = v("cl2"), v("dd"), v("p5", 0, 64)
        ts(v("cl2", 0, 32), v("p5", 128, 160), 0.0, A.is_gt)
        ts(v("cl2", 32, 64), v("p5", 128, 160), 0.0, A.is_gt)
        tt(d, v("SF0"), G2, A.subtract)
        tt(d, d, c2, A.mult)
        tt(v(LAST[t] + "F"), d, G2, A.add)
        if t < 2:
            ts(v("SL"), v("SF", 0, 32), -592.0, A.add)
            ts(v("fxi"), v("SF", 32, 64), 496.0, A.add)
            ts(v("fxi"), v("fxi"), 1023, A.bitwise_and)
            cp(v("FL"), v("fxi"))

    def lists_clause(t):
        d, ch, c2, m = v("cz"), v("CHd" if t < 2 else "HC"), v("cl2"), v("m1")
        ts(d, v("p6", 0, 64), 0.0, A.is_equal)
        tt(d, d, v("p5", 0, 64), A.mult)
        tt(v("CM"), d, v("p6", 0, 64), A.add)
        tt(d, v("NXH"), v("CM"), A.subtract)
        tt(d, d, c2, A.mult)
        tt(ch, d, v("CM"), A.add)
        if t < 2:
            ts(v("CL"), v("CHd", 0, 32), -592.0, A.add)
            ts(v("hb"), v("CHd", 32, 64), -16.0, A.add)
            tt(m, v("CHd", 32, 64), v("IL"), A.is_equal)
            ts(v("eqb"), m, float(-(1 << 23)), A.mult)
            ts(v("HL"), v("CHd", 32, 64), -16.0, A.add)

    def lists_save(t):
        q, c2 = v("tq"), v("cl2")
        tt(v("zz"), v("p6", 64, 128), c2, A.is_gt)
        tt(q, v(LAST[t] + "F"), v("SF0"), A.subtract)
        tt(q, q, v("zz"), A.mult)
        tt(v(LAST[t] + "F0"), v("SF0"), q, A.add)

    def save_c0(t):
        m = v("m1")
        tt(m, v("zz", 0, 32), v("cl2", 0, 32), A.add)
        tt(v("tq", 0, 32), v("CHd" if t < 2 else "HC", 0, 32), v("CP0"), A.subtract)
        tt(m, m, v("tq", 0, 32), A.mult)
        tt(v("CP0" if t < 2 else "HC0"), v("CP0"), m, A.add)

    def next_clash():
        n, s, i = v("nx", 0, 32), v("nx", 32, 64), v("nxi")
        ts(n, v("CP0"), -592.0, A.add)
        ts(s, v("SF0", 0, 32), -592.0, A.add)
        tt(i, n, s, A.mult)
        ts(i, i, 5, A.arith_shift_right)
        ts(n, n, 1.0, A.add)
        tt(i, i, n, A.add)
        ts(i, i, 1023, A.bitwise_and)
        ts(v("NXH", 0, 32), i, 592.0, A.add)

    def send(t, dst_view, src_view, rs, ls):
        dst = T.cores[(rank + t + 1) % len(T.cores)]
        rid, pid, _ = topo.addr(dst)
        k = len(topo.engines(core, dst))
        touch("G", src_view[1], [])
        g.remote_dma(dst_view[0], src_view[0], T.sem[rs], T.sem[ls], pid, rid, topo.mask(core, dst))
        cnt[ls] = k
        note(ls, (ls, k, dict(known["G"])), src_view[1], [])
        src = T.cores[(rank - t - 1) % len(T.cores)]
        cnt[rs] = len(topo.engines(src, core))
        note(rs, (rs, cnt[rs], {}), [], dst_view[1])

    def number_out(j, p, hi, lo):
        mm([(v(p, y, 512, 16, 8), [(v("Ib", y, 128, 16), lo)] + ([(v("Ib", 896 + y, 1024, 16), hi)] if hi else []))
            for y in range(16)])
        act(v("OUT", 512 * j, 512 * j + 512, 1, 8), v(p, 0, 512, 1, 8), F.Copy, float(-592 * 1024 - 16) if hi else -592.0)
        store(T[("yg", "yc", "ysg", "yk")[j]][:], v("OUT", 512 * j, 512 * j + 512, 1, 8))

    def frames_out(a, e):
        y = v("yv", a, e)
        ts(v("lo", a, e), v("oi", a, e), 2047, A.bitwise_and)
        tt(y, v("oi", a, e), v("lo", a, e), A.add)
        act(y, y, F.Relu, v("th2", 4, 5))

    def frames_end(a, e):
        tt(v("yr", a, e), v("yv", a, e), v("p4", a, e), A.add)
        store(T.yf[:, a:e], v("yr", a, e))

    H0, H1 = (0, 256), (256, 512)
    for t in range(3):
        for j in range(2):
            goal(t, 128 * j, 128 * j + 128)
            grec(j)
            if t + j == 0:
                clauses()
        if t == 0:
            constants_a()
        if t:
            lists_save(t - 1)
            save_c0(t - 1)
            for c in (H0, H1):
                clause_a(t, *c)
        clause(t, *H0)
        prep_mm(*H0)
        crec_s(0)
        goal(t, *H1)
        grec(2)
        own_prep(t, *H0)
        clause(t, *H1)
        prep_mm(*H1)
        crec_r(1)
        grec(3)
        if t == 0:
            constants_b()
        keys(t, *CH[0])
        crec(2)
        absd(2)
        crec(3, 0, 64)
        keys_b(t, *CH[0])
        crec(3, 64, 64)
        absd(3, 0, 64)
        if t:
            tt(v("keep"), v("FB", OWN[t], OWN[t] + 512), v("p3"), A.min)
        best(t, *CH[0])
        keys(t, *CH[1])
        absd(3, 64, 64)
        own_prep(t, *H1)
        choose_goal(t, *CH[0])
        own_new(t, *CH[0])
        keys_b(t, *CH[1])
        keys(t, *CH[2])
        best(t, *CH[1])
        next_clash()
        keys_b(t, *CH[2])
        choose_goal(t, *CH[1])
        mm([lsum("p5", 128, "sc", 0, 512)])
        if t == 2:
            frames_out(*CH[0])
        best(t, *CH[2])
        own_new(t, *CH[1])
        choose_goal(t, *CH[2])
        mm([lsum("p5", 0, "Z", 0, 1024)])
        own_new(t, *CH[2])
        lists_goal(t)
        saves()
        if t < 2:
            send(t, v(SLT[t + 1]), v("SL"), "as%d" % t, "ls%d" % t)
            first = (0, 1024)[t]
            o = OWN[t + 1] + 512
            for b, (a, e) in enumerate(MV):
                cp(v("col", a, e), ind(v("FB", first, first + 1024), v("FL", a // 16, e // 16)))
                send(t, v("FB", o + a, o + e), v("col", a, e), "ac%d%d" % (t, b), "lc%d%d" % (t, b))
        else:
            number_out(0, "p1", v("HF", 0, 32), v("HF", 32, 64))
        choose_clause(t, 0, 512)
        mm([lsum("p6", 0, "Z", 1024, 2048)])
        if t < 2:
            mm([(v("p7"), [(ONES, v("sc"))])])
            act(v("ab"), v("p7"), F.Abs, 0.0, 1.0 / 32)
            act(v("ab"), v("ab"), F.Abs, v("th2", 2, 3))
            act(v("a2"), v("ab"), F.Abs, v("th2", 3, 4))
        if t < 2:
            marks(t, 0, 512)
        else:
            frames_out(*H1)
        lists_clause(t)
        if t < 2:
            mm([(v("p1", y, 512, 16), [(v("BY", 128 * y, 128 * y + 128), v("hb")), (v("BY", 128 * y, 128 * y + 128), v("eqb"))]) for y in range(16)])
            act(v("bR"), v("p1"), F.Copy)
            mm([lsum("p6", 64, "zb", 0, 512), lsum("p6", 96, "zb", 0, 512)])
            mm([(v("p3"), [(R1, v("row", 640, 1152, 1, 1)), (IM(6), v("mu"))])])
    mm([lsum("p6", 64, "zb", 0, 512), lsum("p6", 96, "zb", 0, 512)])
    number_out(1, "p7", v("HC", 0, 32), v("HC", 32, 64))
    marks(2, 0, 512)
    lists_save(2)
    save_c0(2)
    number_out(2, "p1", v("HF0", 0, 32), v("HF0", 32, 64))
    number_out(3, "p2", None, v("HC0"))
    frames_end(*H0)
    frames_end(*H1)
    for s in cnt:
        g.wait_ge(T.sem[s], cnt[s])
